import numpy as np
import ml_dtypes


def mxq(x, axis, fmt="e4m3"):
    dtype, down = {"e4m3": (ml_dtypes.float8_e4m3fn, 7), "e5m2": (ml_dtypes.float8_e5m2, 14)}[fmt]
    v = np.moveaxis(np.asarray(x, np.float32).astype(ml_dtypes.bfloat16).astype(np.float64), axis, -1)
    blocks = v.reshape(v.shape[:-1] + (-1, 32))
    amax = np.abs(blocks).max(-1, keepdims=True)
    byte = np.maximum(np.where(amax > 0, np.frexp(amax)[1] - 1 + 127, 0) - down, 1)
    scale = np.exp2(byte - 127.0)
    codes = (blocks / scale).astype(np.float32).astype(dtype).astype(np.float64)
    return np.moveaxis((codes * scale).reshape(v.shape), -1, axis)


WIDE = False


def mx_kscale(k):
    if not WIDE:
        return np.ones(k)
    levels = np.array([10, -10, 5, -5, 0])
    if k % 512:
        return np.exp2(np.random.permutation(np.resize(levels, k // 32))).repeat(32)
    a = np.empty((k // 512, 16))
    for p in range(k // 512):
        a[p, :8] = np.random.permutation(np.resize(levels, 8))
        for g in range(8):
            far = levels[np.abs(levels - a[p, g]) >= 10]
            a[p, g + 8] = far[np.random.randint(len(far))]
    return np.exp2(a.ravel()).repeat(32)


def f64(x):
    return np.asarray(x).astype(np.float64)


def striped(idx):
    return np.tile(idx.reshape(-1, 16).T, (8, 1)).astype(np.uint16)


def unstriped(offs):
    return offs[:16].T.reshape(-1).astype(np.int64)


E2M1 = np.array([0.0, 0.5, 1.0, 1.5, 2.0, 3.0, 4.0, 6.0, -0.0, -0.5, -1.0, -1.5, -2.0, -3.0, -4.0, -6.0])


def pack_fp4(w):
    k, n = w.shape
    w = f64(np.asarray(w, np.float32).astype(ml_dtypes.bfloat16)).reshape(k // 32, 32, n)
    amax = np.abs(w).max(1)
    mant, ex = np.frexp(amax / 6.0)
    byte = np.clip(np.where(amax > 0, np.where(mant > 0.5, ex, ex - 1) + 127, 1), 1, 254)
    scaled = (w * np.exp2(127.0 - byte)[:, None, :]).reshape(k, n).astype(np.float32)
    c = np.ascontiguousarray(scaled.reshape(k // 512, 128, 4, n).transpose(0, 1, 3, 2)).astype(ml_dtypes.float4_e2m1fn).view(np.uint8) & 0xF
    words = (c[..., 0::2] | (c[..., 1::2] << 4)).reshape(k // 512, 128, 2 * n)
    return np.ascontiguousarray(words), np.ascontiguousarray(byte.astype(np.uint8).reshape(k // 512, 16, n))


def unpack_fp4(words, scales):
    g, _, n = scales.shape
    words = np.ascontiguousarray(words).reshape(g, 128, n, 2)
    nib = np.empty((g, 128, n, 4), np.uint8)
    nib[..., 0::2] = words & 0xF
    nib[..., 1::2] = words >> 4
    vals = E2M1[nib] * np.repeat(np.exp2(scales.astype(np.float64) - 127.0), 8, axis=1)[..., None]
    return vals.transpose(0, 1, 3, 2).reshape(g * 512, n)


def sigmoid(v):
    return 1.0 / (1.0 + np.exp(-np.maximum(v, -700.0)))


K, T, S, N, U = 1024, 1024, 512, 256, 1024


def setup_inputs():
    n = np.random.standard_normal
    s = mx_kscale(K)[:, None]
    packed_xT = pack_fp4(n((K, T)) * s)
    return {
        "x_words": packed_xT[0],
        "x_scales": packed_xT[1],
        "mem": n((N, U)).astype(np.float32),
        "w1": (n((K, N)) / np.sqrt(K) / s).astype(np.float32),
        "w2": (n((K, N)) / np.sqrt(K) / s).astype(np.float32),
        "offs": striped(np.random.permutation(T)[:S]),
        "slot": striped(np.random.permutation(U)[:S]),
    }


def reference(x_words, x_scales, mem, w1, w2, offs, slot):
    old = f64(mem)[:, unstriped(slot)]
    xq = unpack_fp4(x_words, x_scales)[:, unstriped(offs)]
    g = sigmoid(mxq(f64(w2), 0, "e4m3").T @ xq)
    y = np.tanh(mxq(f64(w1), 0, "e4m3").T @ xq)
    out = f64(mem).copy()
    out[:, unstriped(slot)] = old + g * (y - old)
    return out

@@ -1,0 +1,136 @@
+from contextlib import ExitStack
+
+import concourse.mybir as mybir
+
+K, T, S, N, U = 1024, 1024, 512, 256, 1024
+FLOPS = 2 * 2 * K * N * S
+
+F32 = mybir.dt.float32
+BF16 = mybir.dt.bfloat16
+I32 = mybir.dt.int32
+U32 = mybir.dt.uint32
+U16 = mybir.dt.uint16
+U8 = mybir.dt.uint8
+FP8X4 = mybir.dt.float8_e4m3fn_x4
+FP4X4 = mybir.dt.float4_e2m1fn_x4
+ACT = mybir.ActivationFunctionType
+ALU = mybir.AluOpType
+
+P = 128
+PACK = 4
+K_PASS = P * PACK
+PASSES = K // K_PASS
+BLOCKS = N // P
+QUAD = 32
+RUN = 4
+
+
+def tile_picked_gmem_tanh_p_kernel(
+    tc, x_words, x_scales, mem, w1, w2, offs, slot, out
+):
+    nc = tc.nc
+    with ExitStack() as ctx:
+        lists = ctx.enter_context(tc.tile_pool(name="lists", bufs=1))
+        keep = ctx.enter_context(tc.tile_pool(name="keep", bufs=1))
+        psum = ctx.enter_context(tc.psum_pool(name="psum", bufs=1))
+
+        offs_sb = lists.tile([P, S // 16], U16, name="offs_sb")
+        slot_sb = lists.tile([P, S // 16], U16, name="slot_sb")
+
+        warm_in = keep.tile([P, 1], F32, name="warm_in")
+        warm_out = keep.tile([P, 1], F32, name="warm_out")
+        scale_table = keep.tile([P, PASSES, T], U8, name="scale_table", align_bytes=64)
+        nc.vector.memset(scale_table[:].rearrange("p z c -> p (z c)").bitcast(I32), 0)
+        nc.gpsimd.memset(warm_in[:], 0.0)
+        nc.scalar.activation(out=warm_out[:], in_=warm_in[:], func=ACT.Sigmoid)
+
+        word_table = [keep.tile([P, T], U16, name="word_table%d" % z, align_bytes=64) for z in range(PASSES)]
+        nc.sync.dma_start(offs_sb[:], offs)
+        nc.sync.dma_start(word_table[0][:].bitcast(I32), x_words[0].bitcast(I32))
+        for q in range(P // QUAD):
+            nc.sync.dma_start(
+                scale_table[QUAD * q : QUAD * q + 4, :, :].bitcast(I32),
+                x_scales[:, 4 * q : 4 * q + 4, :].rearrange("z r c -> r z c").bitcast(I32),
+            )
+        nc.sync.dma_start(word_table[1][:].bitcast(I32), x_words[1].bitcast(I32))
+
+        weights = {"gate": w2, "cand": w1}
+        raw = {}
+        window = [keep.tile([P, U], F32, name="window%d" % b) for b in range(BLOCKS)]
+        for b in range(BLOCKS):
+            for kind in ("gate", "cand"):
+                for z in range(PASSES):
+                    t = keep.tile([P, PACK, P], F32, name="raw_%s%d%d" % (kind, b, z))
+                    rows = weights[kind][z * K_PASS : (z + 1) * K_PASS, b * P : (b + 1) * P]
+                    nc.sync.dma_start(t[:], rows.rearrange("(p j) c -> p j c", j=PACK))
+                    raw[(kind, b, z)] = t
+            if b == 0:
+                nc.sync.dma_start(slot_sb[:], slot)
+            nc.sync.dma_start(window[b][:], mem[b * P : (b + 1) * P, :])
+
+        x_codes = [keep.tile([P, S], U16, name="x_codes%d" % z, align_bytes=64) for z in range(PASSES)]
+        x_plane = [keep.tile([P, S], U8, name="x_plane%d" % z, align_bytes=64) for z in range(PASSES)]
+        for z in range(PASSES):
+            nc.vector.tensor_copy(x_codes[z][:], word_table[z][:].indirect(offs_sb[:]))
+            nc.vector.tensor_copy(x_plane[z][:], scale_table[:, z, :].indirect(offs_sb[:]))
+
+        def quantise(kind, b, z, tag=None):
+            name = "%s%d%d" % (kind, b, z)
+            grouped = keep.tile([P, P * PACK], BF16, name="grouped_" + name, tag=tag or "grouped_" + name, align_bytes=64)
+            nc.scalar.copy(
+                out=grouped[:].rearrange("p (c i j) -> p c j i", i=RUN, j=PACK),
+                in_=raw[(kind, b, z)][:].rearrange("p j (c i) -> p c j i", i=RUN),
+            )
+            codes = keep.tile([P, P], U32, name="codes_" + name, align_bytes=64)
+            plane = keep.tile([P, P], U8, name="plane_" + name, align_bytes=64)
+            nc.vector.quantize_mx(out=codes[:].bitcast(FP8X4), scales=plane[:], in_=grouped[:])
+            return codes, plane
+
+        def product(kind, b, hold=None):
+            acc = psum.tile([P, S], F32, name="acc_%s%d" % (kind, b))
+            for z in range(PASSES):
+                codes, plane = quantise(kind, b, z, hold if z == PASSES - 1 else None)
+                nc.tensor.matmul_mx(
+                    out=acc[:],
+                    lhsT=codes[:].bitcast(FP8X4),
+                    lhsT_scale=plane[:],
+                    rhs=x_codes[z][:].bitcast(FP4X4),
+                    rhs_scale=x_plane[z][:],
+                    start=(z == 0),
+                    stop=(z == PASSES - 1),
+                )
+            return acc
+
+        def activations(b, hold=None):
+            gate_acc = product("gate", b)
+            cand_acc = product("cand", b, hold)
+            stay = keep.tile([P, S], F32, name="stay%d" % b)
+            nc.scalar.activation(out=stay[:], in_=gate_acc[:], func=ACT.Sigmoid, scale=-1.0)
+            neg_cand = keep.tile([P, S], F32, name="neg_cand%d" % b)
+            nc.scalar.activation(out=neg_cand[:], in_=cand_acc[:], func=ACT.Tanh, scale=-1.0)
+            return stay, neg_cand
+
+        def look_up(b, stay):
+            kept = keep.tile([P, S], F32, name="kept%d" % b)
+            nc.vector.tensor_tensor(kept[:], window[b][:].indirect(slot_sb[:]), stay[:], ALU.mult)
+            return kept
+
+        def write_back(b, stay, neg_cand, kept, lo, hi, tag):
+            fresh = keep.tile([P, hi - lo], F32, name="fresh%d_%d" % (b, lo), tag=tag, align_bytes=64)
+            nc.vector.scalar_tensor_tensor(
+                out=fresh[:], in0=stay[:, lo:hi], scalar=1.0, in1=neg_cand[:, lo:hi], op0=ALU.subtract, op1=ALU.mult
+            )
+            nc.vector.tensor_tensor(
+                window[b][:].indirect(slot_sb[:, lo // 16 : hi // 16]), kept[:, lo:hi], fresh[:], ALU.add
+            )
+
+        half = S // 2
+        stay0, neg_cand0 = activations(0)
+        kept0 = look_up(0, stay0)
+        write_back(0, stay0, neg_cand0, kept0, 0, half, "fresh_first")
+        stay1, neg_cand1 = activations(1, "hold")
+        write_back(0, stay0, neg_cand0, kept0, half, S, "hold")
+        nc.sync.dma_start(out[0:P, :], window[0][:])
+        kept1 = look_up(1, stay1)
+        write_back(1, stay1, neg_cand1, kept1, 0, S, "fresh_last")
+        nc.sync.dma_start(out[P : 2 * P, :], window[1][:])

@@ -37,100 +37,117 @@ def tile_picked_gmem_tanh_p_kernel(
         offs_sb = lists.tile([P, S // 16], U16, name="offs_sb")
         slot_sb = lists.tile([P, S // 16], U16, name="slot_sb")
 
-        warm_in = keep.tile([P, 1], F32, name="warm_in")
-        warm_out = keep.tile([P, 1], F32, name="warm_out")
-        scale_table = keep.tile([P, PASSES, T], U8, name="scale_table", align_bytes=64)
-        nc.vector.memset(scale_table[:].rearrange("p z c -> p (z c)").bitcast(I32), 0)
+        scale_table = keep.tile([P, T], U8, name="scale_table", tag="after_scales", align_bytes=64)
+        nc.vector.memset(scale_table[:].bitcast(I32), 0)
+        x_plane = [keep.tile([P, S], U8, name="x_plane%d" % z, align_bytes=64) for z in range(PASSES)]
+        nc.gpsimd.memset(x_plane[1][:].bitcast(I32), 0)
+        warm_in = keep.tile([P, 1], F32, name="warm_in", tag="after_warm_in", align_bytes=64)
+        warm_out = keep.tile([P, 1], F32, name="warm_out", tag="after_warm_out", align_bytes=64)
         nc.gpsimd.memset(warm_in[:], 0.0)
         nc.scalar.activation(out=warm_out[:], in_=warm_in[:], func=ACT.Sigmoid)
 
-        word_table = [keep.tile([P, T], U16, name="word_table%d" % z, align_bytes=64) for z in range(PASSES)]
+        def load_words(z, tag):
+            table = keep.tile([P, T], U16, name="word_table%d" % z, tag=tag, align_bytes=64)
+            nc.sync.dma_start(table[:].bitcast(I32), x_words[z].bitcast(I32))
+            return table
+
+        def load_weights(w, z, dst):
+            nc.sync.dma_start(dst, w[z * K_PASS : (z + 1) * K_PASS, :].rearrange("(p j) c -> p j c", j=PACK))
+            return dst
+
         nc.sync.dma_start(offs_sb[:], offs)
-        nc.sync.dma_start(word_table[0][:].bitcast(I32), x_words[0].bitcast(I32))
+        nc.sync.dma_start(slot_sb[:], slot)
+        word_table = [load_words(0, "word_table0")]
+        raw_first = keep.tile([P, PACK, N], F32, name="raw_first")
+        raw = {("gate", 0): load_weights(w2, 0, raw_first[:])}
         for q in range(P // QUAD):
             nc.sync.dma_start(
-                scale_table[QUAD * q : QUAD * q + 4, :, :].bitcast(I32),
-                x_scales[:, 4 * q : 4 * q + 4, :].rearrange("z r c -> r z c").bitcast(I32),
+                scale_table[QUAD * q : QUAD * q + 4 * PASSES, :].bitcast(I32),
+                x_scales[:, 4 * q : 4 * q + 4, :].bitcast(I32),
             )
-        nc.sync.dma_start(word_table[1][:].bitcast(I32), x_words[1].bitcast(I32))
+        word_table.append(load_words(1, "after_warm_in"))
+        raw_rest = keep.tile([P, 3, PACK, N], F32, name="raw_rest", tag="after_warm_out", align_bytes=64)
+        raw[("gate", 1)] = load_weights(w2, 1, raw_rest[:, 0, :, :])
+        raw[("cand", 0)] = load_weights(w1, 0, raw_rest[:, 1, :, :])
+        raw[("cand", 1)] = load_weights(w1, 1, raw_rest[:, 2, :, :])
 
-        weights = {"gate": w2, "cand": w1}
-        raw = {}
-        window = [keep.tile([P, U], F32, name="window%d" % b) for b in range(BLOCKS)]
-        for b in range(BLOCKS):
-            for kind in ("gate", "cand"):
-                for z in range(PASSES):
-                    t = keep.tile([P, PACK, P], F32, name="raw_%s%d%d" % (kind, b, z))
-                    rows = weights[kind][z * K_PASS : (z + 1) * K_PASS, b * P : (b + 1) * P]
-                    nc.sync.dma_start(t[:], rows.rearrange("(p j) c -> p j c", j=PACK))
-                    raw[(kind, b, z)] = t
-            if b == 0:
-                nc.sync.dma_start(slot_sb[:], slot)
-            nc.sync.dma_start(window[b][:], mem[b * P : (b + 1) * P, :])
-
-        x_codes = [keep.tile([P, S], U16, name="x_codes%d" % z, align_bytes=64) for z in range(PASSES)]
-        x_plane = [keep.tile([P, S], U8, name="x_plane%d" % z, align_bytes=64) for z in range(PASSES)]
-        for z in range(PASSES):
-            nc.vector.tensor_copy(x_codes[z][:], word_table[z][:].indirect(offs_sb[:]))
-            nc.vector.tensor_copy(x_plane[z][:], scale_table[:, z, :].indirect(offs_sb[:]))
-
-        def quantise(kind, b, z, tag=None):
-            name = "%s%d%d" % (kind, b, z)
-            grouped = keep.tile([P, P * PACK], BF16, name="grouped_" + name, tag=tag or "grouped_" + name, align_bytes=64)
-            nc.scalar.copy(
+        def interleave(engine_copy, src, name):
+            grouped = keep.tile([P, src.shape[2] * PACK], BF16, name=name, tag="after_" + name, align_bytes=64)
+            engine_copy(
                 out=grouped[:].rearrange("p (c i j) -> p c j i", i=RUN, j=PACK),
-                in_=raw[(kind, b, z)][:].rearrange("p j (c i) -> p c j i", i=RUN),
+                in_=src.rearrange("p j (c i) -> p c j i", i=RUN),
             )
-            codes = keep.tile([P, P], U32, name="codes_" + name, align_bytes=64)
-            plane = keep.tile([P, P], U8, name="plane_" + name, align_bytes=64)
+            return grouped
+
+        def mx_tiles(name, tag):
+            codes = keep.tile([P, N], U32, name="codes_" + name, tag=tag, align_bytes=64)
+            plane = keep.tile([P, N], U8, name="plane_" + name, align_bytes=64)
+            return codes, plane
+
+        def quantise(kind, z):
+            name = "%s%d" % (kind, z)
+            engine_copy = nc.vector.tensor_copy if (kind, z) == ("cand", PASSES - 1) else nc.scalar.copy
+            grouped = interleave(engine_copy, raw[(kind, z)], "grouped_" + name)
+            codes, plane = mx_tiles(name, "codes_" + name)
             nc.vector.quantize_mx(out=codes[:].bitcast(FP8X4), scales=plane[:], in_=grouped[:])
             return codes, plane
 
-        def product(kind, b, hold=None):
-            acc = psum.tile([P, S], F32, name="acc_%s%d" % (kind, b))
-            for z in range(PASSES):
-                codes, plane = quantise(kind, b, z, hold if z == PASSES - 1 else None)
-                nc.tensor.matmul_mx(
-                    out=acc[:],
-                    lhsT=codes[:].bitcast(FP8X4),
-                    lhsT_scale=plane[:],
-                    rhs=x_codes[z][:].bitcast(FP4X4),
-                    rhs_scale=x_plane[z][:],
-                    start=(z == 0),
-                    stop=(z == PASSES - 1),
-                )
-            return acc
+        x_codes = [keep.tile([P, S], U16, name="x_codes0", align_bytes=64)]
+        nc.vector.tensor_copy(x_codes[0][:], word_table[0][:].indirect(offs_sb[:]))
+        nc.vector.tensor_copy(x_plane[0][:], scale_table[:].indirect(offs_sb[:]))
+        nc.sync.dma_start(x_plane[1][0:112, :].bitcast(I32), x_plane[0][4:116, :].bitcast(I32))
 
-        def activations(b, hold=None):
-            gate_acc = product("gate", b)
-            cand_acc = product("cand", b, hold)
-            stay = keep.tile([P, S], F32, name="stay%d" % b)
-            nc.scalar.activation(out=stay[:], in_=gate_acc[:], func=ACT.Sigmoid, scale=-1.0)
-            neg_cand = keep.tile([P, S], F32, name="neg_cand%d" % b)
-            nc.scalar.activation(out=neg_cand[:], in_=cand_acc[:], func=ACT.Tanh, scale=-1.0)
-            return stay, neg_cand
+        first = mx_tiles("gate0", "after_scales")
+        for b in range(BLOCKS):
+            cols = slice(b * P, (b + 1) * P)
+            grouped = interleave(nc.scalar.copy, raw[("gate", 0)][:, :, cols], "first%d" % b)
+            nc.vector.quantize_mx(out=first[0][:, cols].bitcast(FP8X4), scales=first[1][:, cols], in_=grouped[:])
 
-        def look_up(b, stay):
-            kept = keep.tile([P, S], F32, name="kept%d" % b)
-            nc.vector.tensor_tensor(kept[:], window[b][:].indirect(slot_sb[:]), stay[:], ALU.mult)
-            return kept
+        x_codes.append(keep.tile([P, S], U16, name="x_codes1", tag="after_first1", align_bytes=64))
+        nc.vector.tensor_copy(x_codes[1][:], word_table[1][:].indirect(offs_sb[:]))
 
-        def write_back(b, stay, neg_cand, kept, lo, hi, tag):
-            fresh = keep.tile([P, hi - lo], F32, name="fresh%d_%d" % (b, lo), tag=tag, align_bytes=64)
+        def products(kind, func, operands):
+            result = keep.tile([P, BLOCKS * S], F32, name="result_" + kind)
+            for b in range(BLOCKS):
+                acc = psum.tile([P, S], F32, name="acc_%s%d" % (kind, b))
+                for z, (codes, plane) in enumerate(operands):
+                    nc.tensor.matmul_mx(
+                        out=acc[:],
+                        lhsT=codes[:, b * P : (b + 1) * P].bitcast(FP8X4),
+                        lhsT_scale=plane[:, b * P : (b + 1) * P],
+                        rhs=x_codes[z][:].bitcast(FP4X4),
+                        rhs_scale=x_plane[z][:],
+                        start=(z == 0),
+                        stop=(z == PASSES - 1),
+                    )
+                nc.scalar.activation(out=result[:, b * S : (b + 1) * S], in_=acc[:], func=func, scale=-1.0)
+            return result
+
+        def load_memory(b, tag):
+            tile = keep.tile([P, U], F32, name="window%d" % b, tag=tag, align_bytes=64)
+            nc.sync.dma_start(tile[:], mem[b * P : (b + 1) * P, :])
+            return tile
+
+        window = [load_memory(0, "after_first0"), load_memory(1, "after_warm_in")]
+        stay = products("gate", ACT.Sigmoid, [first, quantise("gate", 1)])
+        neg_cand = products("cand", ACT.Tanh, [quantise("cand", z) for z in range(PASSES)])
+
+        kept = keep.tile([P, BLOCKS * S], F32, name="kept")
+        for b in range(BLOCKS):
+            cols = slice(b * S, (b + 1) * S)
+            nc.vector.tensor_tensor(kept[:, cols], window[b][:].indirect(slot_sb[:]), stay[:, cols], ALU.mult)
+        fresh = keep.tile([P, BLOCKS * S], F32, name="fresh")
+        for b in range(BLOCKS):
+            cols = slice(b * S, (b + 1) * S)
             nc.vector.scalar_tensor_tensor(
-                out=fresh[:], in0=stay[:, lo:hi], scalar=1.0, in1=neg_cand[:, lo:hi], op0=ALU.subtract, op1=ALU.mult
+                out=fresh[:, cols],
+                in0=stay[:, cols],
+                scalar=1.0,
+                in1=neg_cand[:, cols],
+                op0=ALU.subtract,
+                op1=ALU.mult,
             )
-            nc.vector.tensor_tensor(
-                window[b][:].indirect(slot_sb[:, lo // 16 : hi // 16]), kept[:, lo:hi], fresh[:], ALU.add
-            )
-
-        half = S // 2
-        stay0, neg_cand0 = activations(0)
-        kept0 = look_up(0, stay0)
-        write_back(0, stay0, neg_cand0, kept0, 0, half, "fresh_first")
-        stay1, neg_cand1 = activations(1, "hold")
-        write_back(0, stay0, neg_cand0, kept0, half, S, "hold")
-        nc.sync.dma_start(out[0:P, :], window[0][:])
-        kept1 = look_up(1, stay1)
-        write_back(1, stay1, neg_cand1, kept1, 0, S, "fresh_last")
-        nc.sync.dma_start(out[P : 2 * P, :], window[1][:])
+        for b in range(BLOCKS):
+            cols = slice(b * S, (b + 1) * S)
+            nc.vector.tensor_tensor(window[b][:].indirect(slot_sb[:]), kept[:, cols], fresh[:, cols], ALU.add)
+            nc.sync.dma_start(out[b * P : (b + 1) * P, :], window[b][:])

@@ -43,7 +43,7 @@ def tile_picked_gmem_tanh_p_kernel(
         nc.gpsimd.memset(x_plane[1][:].bitcast(I32), 0)
         warm_in = keep.tile([P, 1], F32, name="warm_in", tag="after_warm_in", align_bytes=64)
         warm_out = keep.tile([P, 1], F32, name="warm_out", tag="after_warm_out", align_bytes=64)
-        nc.gpsimd.memset(warm_in[:], 0.0)
+        nc.vector.memset(warm_in[:], 0.0)
         nc.scalar.activation(out=warm_out[:], in_=warm_in[:], func=ACT.Sigmoid)
 
         def load_words(z, tag):
@@ -86,8 +86,16 @@ def tile_picked_gmem_tanh_p_kernel(
 
         def quantise(kind, z):
             name = "%s%d" % (kind, z)
-            engine_copy = nc.vector.tensor_copy if (kind, z) == ("cand", PASSES - 1) else nc.scalar.copy
-            grouped = interleave(engine_copy, raw[(kind, z)], "grouped_" + name)
+            grouped = keep.tile([P, N * PACK], BF16, name="grouped_" + name, align_bytes=64)
+            if (kind, z) == ("cand", PASSES - 1):
+                shares = [(nc.vector.tensor_copy, 0, N)]
+            else:
+                shares = [(nc.scalar.copy, b * P, (b + 1) * P) for b in range(BLOCKS)]
+            for engine_copy, lo, hi in shares:
+                engine_copy(
+                    out=grouped[:, lo * PACK : hi * PACK].rearrange("p (c i j) -> p c j i", i=RUN, j=PACK),
+                    in_=raw[(kind, z)][:, :, lo:hi].rearrange("p j (c i) -> p c j i", i=RUN),
+                )
             codes, plane = mx_tiles(name, "codes_" + name)
             nc.vector.quantize_mx(out=codes[:].bitcast(FP8X4), scales=plane[:], in_=grouped[:])
             return codes, plane

@@ -37,125 +37,134 @@ def tile_picked_gmem_tanh_p_kernel(
         offs_sb = lists.tile([P, S // 16], U16, name="offs_sb")
         slot_sb = lists.tile([P, S // 16], U16, name="slot_sb")
 
-        scale_table = keep.tile([P, T], U8, name="scale_table", tag="after_scales", align_bytes=64)
-        nc.vector.memset(scale_table[:].bitcast(I32), 0)
-        x_plane = [keep.tile([P, S], U8, name="x_plane%d" % z, align_bytes=64) for z in range(PASSES)]
-        nc.gpsimd.memset(x_plane[1][:].bitcast(I32), 0)
-        warm_in = keep.tile([P, 1], F32, name="warm_in", tag="after_warm_in", align_bytes=64)
-        warm_out = keep.tile([P, 1], F32, name="warm_out", tag="after_warm_out", align_bytes=64)
-        nc.vector.memset(warm_in[:], 0.0)
-        nc.scalar.activation(out=warm_out[:], in_=warm_in[:], func=ACT.Sigmoid)
+        def sbuf(shape, dtype, name, after=None):
+            return keep.tile(shape, dtype, name=name, tag=after or name, align_bytes=64)
 
-        def load_words(z, tag):
-            table = keep.tile([P, T], U16, name="word_table%d" % z, tag=tag, align_bytes=64)
+        def load_words(z, after=None):
+            table = sbuf([P, T], U16, "word_table%d" % z, after)
             nc.sync.dma_start(table[:].bitcast(I32), x_words[z].bitcast(I32))
             return table
 
-        def load_weights(w, z, dst):
-            nc.sync.dma_start(dst, w[z * K_PASS : (z + 1) * K_PASS, :].rearrange("(p j) c -> p j c", j=PACK))
-            return dst
+        def load_weights(w, z, name, after=None):
+            raw = sbuf([P, PACK, N], F32, name, after)
+            nc.sync.dma_start(raw[:], w[z * K_PASS : (z + 1) * K_PASS, :].rearrange("(p j) c -> p j c", j=PACK))
+            return raw
+
+        def load_memory(b, after=None):
+            window = sbuf([P, U], F32, "window%d" % b, after)
+            nc.sync.dma_start(window[:], mem[b * P : (b + 1) * P, :])
+            return window
+
+        def interleave(engine_copy, raw, grouped, lo, hi):
+            engine_copy(
+                out=grouped[:, lo * PACK : hi * PACK].rearrange("p (c i j) -> p c j i", i=RUN, j=PACK),
+                in_=raw[:, :, lo:hi].rearrange("p j (c i) -> p c j i", i=RUN),
+            )
+
+        def quantise(grouped, operand, lo, hi):
+            codes, plane = operand
+            nc.vector.quantize_mx(
+                out=codes[:, lo:hi].bitcast(FP8X4), scales=plane[:, lo:hi], in_=grouped[:, lo * PACK : hi * PACK]
+            )
+
+        def mx_tiles(name, after=None):
+            return sbuf([P, N], U32, "codes_" + name, after), sbuf([P, N], U8, "plane_" + name)
+
+        def product(kind, b, operands, func, result):
+            acc = psum.tile([P, S], F32, name="acc_%s%d" % (kind, b))
+            for z, (codes, plane) in enumerate(operands):
+                nc.tensor.matmul_mx(
+                    out=acc[:],
+                    lhsT=codes[:, b * P : (b + 1) * P].bitcast(FP8X4),
+                    lhsT_scale=plane[:, b * P : (b + 1) * P],
+                    rhs=x_codes[z][:].bitcast(FP4X4),
+                    rhs_scale=x_plane[z][:],
+                    start=(z == 0),
+                    stop=(z == PASSES - 1),
+                )
+            nc.scalar.activation(out=result[:], in_=acc[:], func=func, scale=-1.0)
+
+        shared = ctx.enter_context(tc.tile_pool(name="shared", bufs=1))
+        scale_table = shared.tile([P, T], U8, name="scale_table", offset=4 * U - T // 2, align_bytes=64)
+        nc.vector.memset(scale_table[:].bitcast(I32), 0)
+        x_plane = [sbuf([P, S], U8, "x_plane%d" % z) for z in range(PASSES)]
+        nc.gpsimd.memset(x_plane[1][:].bitcast(I32), 0)
+        warm_in = sbuf([P, 1], F32, "warm_in")
+        warm_out = sbuf([P, 1], F32, "warm_out")
+        nc.vector.memset(warm_in[:], 0.0)
+        nc.scalar.activation(out=warm_out[:], in_=warm_in[:], func=ACT.Sigmoid)
 
         nc.sync.dma_start(offs_sb[:], offs)
         nc.sync.dma_start(slot_sb[:], slot)
-        word_table = [load_words(0, "word_table0")]
-        raw_first = keep.tile([P, PACK, N], F32, name="raw_first")
-        raw = {("gate", 0): load_weights(w2, 0, raw_first[:])}
-        for q in range(P // QUAD):
+        word_table = [load_words(0)]
+        raw_gate = [load_weights(w2, 0, "raw_gate0")]
+        for r in range(4):
             nc.sync.dma_start(
-                scale_table[QUAD * q : QUAD * q + 4 * PASSES, :].bitcast(I32),
-                x_scales[:, 4 * q : 4 * q + 4, :].bitcast(I32),
+                scale_table[r:P:16, :].bitcast(I32),
+                x_scales.rearrange("z (q r) c -> r q z c", r=4)[r].bitcast(I32),
             )
-        word_table.append(load_words(1, "after_warm_in"))
-        raw_rest = keep.tile([P, 3, PACK, N], F32, name="raw_rest", tag="after_warm_out", align_bytes=64)
-        raw[("gate", 1)] = load_weights(w2, 1, raw_rest[:, 0, :, :])
-        raw[("cand", 0)] = load_weights(w1, 0, raw_rest[:, 1, :, :])
-        raw[("cand", 1)] = load_weights(w1, 1, raw_rest[:, 2, :, :])
-
-        def interleave(engine_copy, src, name):
-            grouped = keep.tile([P, src.shape[2] * PACK], BF16, name=name, tag="after_" + name, align_bytes=64)
-            engine_copy(
-                out=grouped[:].rearrange("p (c i j) -> p c j i", i=RUN, j=PACK),
-                in_=src.rearrange("p j (c i) -> p c j i", i=RUN),
+        word_table.append(load_words(1, "warm_in"))
+        raw_next = sbuf([P, 3, PACK, N], F32, "raw_next", "warm_out")
+        for i, (w, z) in enumerate(((w2, 1), (w1, 0), (w1, 1))):
+            nc.sync.dma_start(
+                raw_next[:, i, :, :], w[z * K_PASS : (z + 1) * K_PASS, :].rearrange("(p j) c -> p j c", j=PACK)
             )
-            return grouped
+        raw_gate.append(raw_next[:, 0, :, :])
+        raw_cand = [raw_next[:, 1, :, :], raw_next[:, 2, :, :]]
 
-        def mx_tiles(name, tag):
-            codes = keep.tile([P, N], U32, name="codes_" + name, tag=tag, align_bytes=64)
-            plane = keep.tile([P, N], U8, name="plane_" + name, align_bytes=64)
-            return codes, plane
-
-        def quantise(kind, z):
-            name = "%s%d" % (kind, z)
-            grouped = keep.tile([P, N * PACK], BF16, name="grouped_" + name, align_bytes=64)
-            if (kind, z) == ("cand", PASSES - 1):
-                shares = [(nc.vector.tensor_copy, 0, N)]
-            else:
-                shares = [(nc.scalar.copy, b * P, (b + 1) * P) for b in range(BLOCKS)]
-            for engine_copy, lo, hi in shares:
-                engine_copy(
-                    out=grouped[:, lo * PACK : hi * PACK].rearrange("p (c i j) -> p c j i", i=RUN, j=PACK),
-                    in_=raw[(kind, z)][:, :, lo:hi].rearrange("p j (c i) -> p c j i", i=RUN),
-                )
-            codes, plane = mx_tiles(name, "codes_" + name)
-            nc.vector.quantize_mx(out=codes[:].bitcast(FP8X4), scales=plane[:], in_=grouped[:])
-            return codes, plane
-
-        x_codes = [keep.tile([P, S], U16, name="x_codes0", align_bytes=64)]
+        x_codes = [sbuf([P, S], U16, "x_codes0")]
         nc.vector.tensor_copy(x_codes[0][:], word_table[0][:].indirect(offs_sb[:]))
         nc.vector.tensor_copy(x_plane[0][:], scale_table[:].indirect(offs_sb[:]))
-        nc.sync.dma_start(x_plane[1][0:112, :].bitcast(I32), x_plane[0][4:116, :].bitcast(I32))
+        nc.sync.dma_start(x_plane[1][0:112, :].bitcast(I32), x_plane[0][16:128, :].bitcast(I32))
+        window = [shared.tile([P, U], F32, name="window0", offset=0, align_bytes=64)]
+        nc.sync.dma_start(window[0][:], mem[0:P, :])
 
-        first = mx_tiles("gate0", "after_scales")
+        operand = {}
+        operand["gate", 0] = (
+            shared.tile([P, N], U32, name="codes_gate0", offset=4 * U, align_bytes=64),
+            sbuf([P, N], U8, "plane_gate0"),
+        )
         for b in range(BLOCKS):
-            cols = slice(b * P, (b + 1) * P)
-            grouped = interleave(nc.scalar.copy, raw[("gate", 0)][:, :, cols], "first%d" % b)
-            nc.vector.quantize_mx(out=first[0][:, cols].bitcast(FP8X4), scales=first[1][:, cols], in_=grouped[:])
-
-        x_codes.append(keep.tile([P, S], U16, name="x_codes1", tag="after_first1", align_bytes=64))
+            first = sbuf([P, P * PACK], BF16, "first%d" % b)
+            interleave(nc.scalar.copy, raw_gate[0][:, :, b * P : (b + 1) * P], first, 0, P)
+            codes, plane = operand["gate", 0]
+            nc.vector.quantize_mx(
+                out=codes[:, b * P : (b + 1) * P].bitcast(FP8X4), scales=plane[:, b * P : (b + 1) * P], in_=first[:]
+            )
+        x_codes.append(sbuf([P, S], U16, "x_codes1", "first1"))
         nc.vector.tensor_copy(x_codes[1][:], word_table[1][:].indirect(offs_sb[:]))
+        window.append(load_memory(1, "first0"))
 
-        def products(kind, func, operands):
-            result = keep.tile([P, BLOCKS * S], F32, name="result_" + kind)
-            for b in range(BLOCKS):
-                acc = psum.tile([P, S], F32, name="acc_%s%d" % (kind, b))
-                for z, (codes, plane) in enumerate(operands):
-                    nc.tensor.matmul_mx(
-                        out=acc[:],
-                        lhsT=codes[:, b * P : (b + 1) * P].bitcast(FP8X4),
-                        lhsT_scale=plane[:, b * P : (b + 1) * P],
-                        rhs=x_codes[z][:].bitcast(FP4X4),
-                        rhs_scale=x_plane[z][:],
-                        start=(z == 0),
-                        stop=(z == PASSES - 1),
-                    )
-                nc.scalar.activation(out=result[:, b * S : (b + 1) * S], in_=acc[:], func=func, scale=-1.0)
-            return result
-
-        def load_memory(b, tag):
-            tile = keep.tile([P, U], F32, name="window%d" % b, tag=tag, align_bytes=64)
-            nc.sync.dma_start(tile[:], mem[b * P : (b + 1) * P, :])
-            return tile
-
-        window = [load_memory(0, "after_first0"), load_memory(1, "after_warm_in")]
-        stay = products("gate", ACT.Sigmoid, [first, quantise("gate", 1)])
-        neg_cand = products("cand", ACT.Tanh, [quantise("cand", z) for z in range(PASSES)])
-
-        kept = keep.tile([P, BLOCKS * S], F32, name="kept")
+        grouped = {}
+        for kind, z in (("gate", 1), ("cand", 0), ("cand", 1)):
+            grouped[kind, z] = sbuf([P, N * PACK], BF16, "grouped_%s%d" % (kind, z))
+            operand[kind, z] = mx_tiles("%s%d" % (kind, z))
         for b in range(BLOCKS):
-            cols = slice(b * S, (b + 1) * S)
-            nc.vector.tensor_tensor(kept[:, cols], window[b][:].indirect(slot_sb[:]), stay[:, cols], ALU.mult)
-        fresh = keep.tile([P, BLOCKS * S], F32, name="fresh")
+            interleave(nc.scalar.copy, raw_gate[1], grouped["gate", 1], b * P, (b + 1) * P)
+        quantise(grouped["gate", 1], operand["gate", 1], 0, N)
         for b in range(BLOCKS):
-            cols = slice(b * S, (b + 1) * S)
+            interleave(nc.scalar.copy, raw_cand[0], grouped["cand", 0], b * P, (b + 1) * P)
+        quantise(grouped["cand", 0], operand["cand", 0], 0, N)
+
+        stay = [sbuf([P, S], F32, "stay%d" % b) for b in range(BLOCKS)]
+        neg_cand = [sbuf([P, S], F32, "neg_cand%d" % b) for b in range(BLOCKS)]
+        for b in range(BLOCKS):
+            product("gate", b, [operand["gate", z] for z in range(PASSES)], ACT.Sigmoid, stay[b])
+        for b in range(BLOCKS):
+            interleave(nc.vector.tensor_copy, raw_cand[1], grouped["cand", 1], b * P, (b + 1) * P)
+        for b in range(BLOCKS):
+            quantise(grouped["cand", 1], operand["cand", 1], b * P, (b + 1) * P)
+        for b in range(BLOCKS):
+            product("cand", b, [operand["cand", z] for z in range(PASSES)], ACT.Tanh, neg_cand[b])
+
+        kept = [sbuf([P, S], F32, "kept%d" % b) for b in range(BLOCKS)]
+        fresh = [sbuf([P, S], F32, "fresh%d" % b) for b in range(BLOCKS)]
+        for b in range(BLOCKS):
+            nc.vector.tensor_tensor(kept[b][:], window[b][:].indirect(slot_sb[:]), stay[b][:], ALU.mult)
+        for b in range(BLOCKS):
             nc.vector.scalar_tensor_tensor(
-                out=fresh[:, cols],
-                in0=stay[:, cols],
-                scalar=1.0,
-                in1=neg_cand[:, cols],
-                op0=ALU.subtract,
-                op1=ALU.mult,
+                out=fresh[b][:], in0=stay[b][:], scalar=1.0, in1=neg_cand[b][:], op0=ALU.subtract, op1=ALU.mult
             )
         for b in range(BLOCKS):
-            cols = slice(b * S, (b + 1) * S)
-            nc.vector.tensor_tensor(window[b][:].indirect(slot_sb[:]), kept[:, cols], fresh[:, cols], ALU.add)
+            nc.vector.tensor_tensor(window[b][:].indirect(slot_sb[:]), kept[b][:], fresh[b][:], ALU.add)
             nc.sync.dma_start(out[b * P : (b + 1) * P, :], window[b][:])

@@ -71,12 +71,13 @@ def tile_picked_gmem_tanh_p_kernel(
             return sbuf([P, N], U32, "codes_" + name, after), sbuf([P, N], U8, "plane_" + name)
 
         def product(kind, b, operands, func, result):
-            acc = psum.tile([P, S], F32, name="acc_%s%d" % (kind, b))
+            bank = "acc_gate0" if (kind, b) == ("cand", 1) else "acc_%s%d" % (kind, b)
+            acc = psum.tile([P, S], F32, name="acc_%s%d" % (kind, b), tag=bank)
             for z, (codes, plane) in enumerate(operands):
                 nc.tensor.matmul_mx(
                     out=acc[:],
-                    lhsT=codes[:, b * P : (b + 1) * P].bitcast(FP8X4),
-                    lhsT_scale=plane[:, b * P : (b + 1) * P],
+                    lhsT=codes.bitcast(FP8X4),
+                    lhsT_scale=plane,
                     rhs=x_codes[z][:].bitcast(FP4X4),
                     rhs_scale=x_plane[z][:],
                     start=(z == 0),
@@ -84,78 +85,82 @@ def tile_picked_gmem_tanh_p_kernel(
                 )
             nc.scalar.activation(out=result[:], in_=acc[:], func=func, scale=-1.0)
 
-        shared = ctx.enter_context(tc.tile_pool(name="shared", bufs=1))
-        scale_table = shared.tile([P, T], U8, name="scale_table", offset=4 * U - T // 2, align_bytes=64)
+        scale_table = sbuf([P, T], U8, "scale_table")
         nc.vector.memset(scale_table[:].bitcast(I32), 0)
         x_plane = [sbuf([P, S], U8, "x_plane%d" % z) for z in range(PASSES)]
-        nc.gpsimd.memset(x_plane[1][:].bitcast(I32), 0)
+        zeros = sbuf([P, S // 4], I32, "zeros")
+        nc.vector.memset(zeros[:], 0)
+        nc.vector.tensor_copy(x_plane[1][:].bitcast(I32), zeros[:])
         warm_in = sbuf([P, 1], F32, "warm_in")
         warm_out = sbuf([P, 1], F32, "warm_out")
-        nc.vector.memset(warm_in[:], 0.0)
+        nc.gpsimd.memset(warm_in[:], 0.0)
         nc.scalar.activation(out=warm_out[:], in_=warm_in[:], func=ACT.Sigmoid)
 
         nc.sync.dma_start(offs_sb[:], offs)
         nc.sync.dma_start(slot_sb[:], slot)
         word_table = [load_words(0)]
-        raw_gate = [load_weights(w2, 0, "raw_gate0")]
-        for r in range(4):
+        for q in range(P // QUAD):
             nc.sync.dma_start(
-                scale_table[r:P:16, :].bitcast(I32),
-                x_scales.rearrange("z (q r) c -> r q z c", r=4)[r].bitcast(I32),
+                scale_table[QUAD * q : QUAD * q + 4 * PASSES, :].bitcast(I32),
+                x_scales[:, 4 * q : 4 * q + 4, :].bitcast(I32),
             )
+        raw = {("gate", 0): load_weights(w2, 0, "raw_gate0", "zeros")}
         word_table.append(load_words(1, "warm_in"))
         raw_next = sbuf([P, 3, PACK, N], F32, "raw_next", "warm_out")
-        for i, (w, z) in enumerate(((w2, 1), (w1, 0), (w1, 1))):
-            nc.sync.dma_start(
-                raw_next[:, i, :, :], w[z * K_PASS : (z + 1) * K_PASS, :].rearrange("(p j) c -> p j c", j=PACK)
-            )
-        raw_gate.append(raw_next[:, 0, :, :])
-        raw_cand = [raw_next[:, 1, :, :], raw_next[:, 2, :, :]]
+        for i, (kind, w, z) in enumerate((("cand", w1, 0), ("gate", w2, 1), ("cand", w1, 1))):
+            raw[kind, z] = raw_next[:, i, :, :]
+            nc.sync.dma_start(raw[kind, z], w[z * K_PASS : (z + 1) * K_PASS, :].rearrange("(p j) c -> p j c", j=PACK))
 
         x_codes = [sbuf([P, S], U16, "x_codes0")]
         nc.vector.tensor_copy(x_codes[0][:], word_table[0][:].indirect(offs_sb[:]))
         nc.vector.tensor_copy(x_plane[0][:], scale_table[:].indirect(offs_sb[:]))
-        nc.sync.dma_start(x_plane[1][0:112, :].bitcast(I32), x_plane[0][16:128, :].bitcast(I32))
-        window = [shared.tile([P, U], F32, name="window0", offset=0, align_bytes=64)]
-        nc.sync.dma_start(window[0][:], mem[0:P, :])
+        for lo, hi in ((0, 64), (64, 96), (96, 100)):
+            nc.sync.dma_start(x_plane[1][lo:hi, :].bitcast(I32), x_plane[0][4 + lo : 4 + hi, :].bitcast(I32))
 
         operand = {}
-        operand["gate", 0] = (
-            shared.tile([P, N], U32, name="codes_gate0", offset=4 * U, align_bytes=64),
-            sbuf([P, N], U8, "plane_gate0"),
-        )
-        for b in range(BLOCKS):
-            first = sbuf([P, P * PACK], BF16, "first%d" % b)
-            interleave(nc.scalar.copy, raw_gate[0][:, :, b * P : (b + 1) * P], first, 0, P)
-            codes, plane = operand["gate", 0]
-            nc.vector.quantize_mx(
-                out=codes[:, b * P : (b + 1) * P].bitcast(FP8X4), scales=plane[:, b * P : (b + 1) * P], in_=first[:]
-            )
-        x_codes.append(sbuf([P, S], U16, "x_codes1", "first1"))
-        nc.vector.tensor_copy(x_codes[1][:], word_table[1][:].indirect(offs_sb[:]))
-        window.append(load_memory(1, "first0"))
 
-        grouped = {}
-        for kind, z in (("gate", 1), ("cand", 0), ("cand", 1)):
-            grouped[kind, z] = sbuf([P, N * PACK], BF16, "grouped_%s%d" % (kind, z))
-            operand[kind, z] = mx_tiles("%s%d" % (kind, z))
+        def group(engine_copy, kind, z, b):
+            grouped = sbuf([P, P * PACK], BF16, "grouped_%s%d%d" % (kind, z, b))
+            interleave(engine_copy, raw[kind, z][:, :, b * P : (b + 1) * P], grouped, 0, P)
+            return grouped
+
+        def quantise_pass(copies, kind, z):
+            grouped = sbuf([P, N * PACK], BF16, "grouped_%s%d" % (kind, z))
+            for b in range(BLOCKS):
+                interleave(copies[b], raw[kind, z], grouped, b * P, (b + 1) * P)
+            codes, plane = mx_tiles("%s%d" % (kind, z))
+            quantise(grouped, (codes, plane), 0, N)
+            for b in range(BLOCKS):
+                operand[kind, z, b] = (codes[:, b * P : (b + 1) * P], plane[:, b * P : (b + 1) * P])
+
+        def quantise_block(grouped, kind, z, b, after=None):
+            codes = sbuf([P, P], U32, "codes_%s%d%d" % (kind, z, b), after)
+            plane = sbuf([P, P], U8, "plane_%s%d%d" % (kind, z, b))
+            nc.vector.quantize_mx(out=codes[:].bitcast(FP8X4), scales=plane[:], in_=grouped[:])
+            operand[kind, z, b] = (codes[:], plane[:])
+
+        first = [group(nc.scalar.copy, "gate", 0, b) for b in range(BLOCKS)]
+        quantise_block(first[0], "gate", 0, 0, "scale_table")
+        quantise_block(first[1], "gate", 0, 1)
+        window = [load_memory(0, "grouped_gate00")]
+        x_codes.append(sbuf([P, S], U16, "x_codes1", "grouped_gate01"))
+        nc.vector.tensor_copy(x_codes[1][:], word_table[1][:].indirect(offs_sb[:]))
+        window.append(load_memory(1, "warm_in"))
+
+        quantise_pass([nc.scalar.copy, nc.scalar.copy], "cand", 0)
+        second = [group(nc.scalar.copy, "gate", 1, 0), group(nc.scalar.copy, "gate", 1, 1)]
         for b in range(BLOCKS):
-            interleave(nc.scalar.copy, raw_gate[1], grouped["gate", 1], b * P, (b + 1) * P)
-        quantise(grouped["gate", 1], operand["gate", 1], 0, N)
-        for b in range(BLOCKS):
-            interleave(nc.scalar.copy, raw_cand[0], grouped["cand", 0], b * P, (b + 1) * P)
-        quantise(grouped["cand", 0], operand["cand", 0], 0, N)
+            quantise_block(second[b], "gate", 1, b)
 
         stay = [sbuf([P, S], F32, "stay%d" % b) for b in range(BLOCKS)]
         neg_cand = [sbuf([P, S], F32, "neg_cand%d" % b) for b in range(BLOCKS)]
         for b in range(BLOCKS):
-            product("gate", b, [operand["gate", z] for z in range(PASSES)], ACT.Sigmoid, stay[b])
+            product("gate", b, [operand["gate", z, b] for z in range(PASSES)], ACT.Sigmoid, stay[b])
+        last = [group(nc.vector.tensor_copy, "cand", 1, b) for b in range(BLOCKS)]
+        quantise_block(last[0], "cand", 1, 0, "codes_gate10")
+        quantise_block(last[1], "cand", 1, 1, "plane_gate10")
         for b in range(BLOCKS):
-            interleave(nc.vector.tensor_copy, raw_cand[1], grouped["cand", 1], b * P, (b + 1) * P)
-        for b in range(BLOCKS):
-            quantise(grouped["cand", 1], operand["cand", 1], b * P, (b + 1) * P)
-        for b in range(BLOCKS):
-            product("cand", b, [operand["cand", z] for z in range(PASSES)], ACT.Tanh, neg_cand[b])
+            product("cand", b, [operand["cand", z, b] for z in range(PASSES)], ACT.Tanh, neg_cand[b])
 
         kept = [sbuf([P, S], F32, "kept%d" % b) for b in range(BLOCKS)]
         fresh = [sbuf([P, S], F32, "fresh%d" % b) for b in range(BLOCKS)]

@@ -71,8 +71,7 @@ def tile_picked_gmem_tanh_p_kernel(
             return sbuf([P, N], U32, "codes_" + name, after), sbuf([P, N], U8, "plane_" + name)
 
         def product(kind, b, operands, func, result):
-            bank = "acc_gate0" if (kind, b) == ("cand", 1) else "acc_%s%d" % (kind, b)
-            acc = psum.tile([P, S], F32, name="acc_%s%d" % (kind, b), tag=bank)
+            acc = psum.tile([P, S], F32, name="acc_%s%d" % (kind, b))
             for z, (codes, plane) in enumerate(operands):
                 nc.tensor.matmul_mx(
                     out=acc[:],
@@ -85,37 +84,35 @@ def tile_picked_gmem_tanh_p_kernel(
                 )
             nc.scalar.activation(out=result[:], in_=acc[:], func=func, scale=-1.0)
 
-        scale_table = sbuf([P, T], U8, "scale_table")
+        scale_table = sbuf([P, PASSES * T], U8, "scale_table")
         nc.vector.memset(scale_table[:].bitcast(I32), 0)
-        x_plane = [sbuf([P, S], U8, "x_plane%d" % z) for z in range(PASSES)]
-        zeros = sbuf([P, S // 4], I32, "zeros")
-        nc.vector.memset(zeros[:], 0)
-        nc.vector.tensor_copy(x_plane[1][:].bitcast(I32), zeros[:])
+        x_plane = [sbuf([P, S], U8, "x_plane0")]
         warm_in = sbuf([P, 1], F32, "warm_in")
         warm_out = sbuf([P, 1], F32, "warm_out")
-        nc.gpsimd.memset(warm_in[:], 0.0)
+        nc.vector.memset(warm_in[:], 0.0)
         nc.scalar.activation(out=warm_out[:], in_=warm_in[:], func=ACT.Sigmoid)
 
         nc.sync.dma_start(offs_sb[:], offs)
+        word_table = [load_words(z) for z in range(PASSES)]
+        shared = ctx.enter_context(tc.tile_pool(name="shared", bufs=1))
+        raw_first = shared.tile([P, PACK, N], F32, name="raw_gate0", offset=2 * U, align_bytes=64)
+        nc.sync.dma_start(raw_first[:], w2[:K_PASS, :].rearrange("(p j) c -> p j c", j=PACK))
+        raw = {("gate", 0): raw_first}
         nc.sync.dma_start(slot_sb[:], slot)
-        word_table = [load_words(0)]
         for q in range(P // QUAD):
             nc.sync.dma_start(
-                scale_table[QUAD * q : QUAD * q + 4 * PASSES, :].bitcast(I32),
-                x_scales[:, 4 * q : 4 * q + 4, :].bitcast(I32),
+                scale_table[QUAD * q : QUAD * q + 4, :].bitcast(I32).rearrange("r (z c) -> r z c", z=PASSES),
+                x_scales[:, 4 * q : 4 * q + 4, :].bitcast(I32).rearrange("z r c -> r z c"),
             )
-        raw = {("gate", 0): load_weights(w2, 0, "raw_gate0", "zeros")}
-        word_table.append(load_words(1, "warm_in"))
         raw_next = sbuf([P, 3, PACK, N], F32, "raw_next", "warm_out")
-        for i, (kind, w, z) in enumerate((("cand", w1, 0), ("gate", w2, 1), ("cand", w1, 1))):
+        for i, (kind, w, z) in enumerate((("gate", w2, 1), ("cand", w1, 0), ("cand", w1, 1))):
             raw[kind, z] = raw_next[:, i, :, :]
             nc.sync.dma_start(raw[kind, z], w[z * K_PASS : (z + 1) * K_PASS, :].rearrange("(p j) c -> p j c", j=PACK))
 
-        x_codes = [sbuf([P, S], U16, "x_codes0")]
-        nc.vector.tensor_copy(x_codes[0][:], word_table[0][:].indirect(offs_sb[:]))
-        nc.vector.tensor_copy(x_plane[0][:], scale_table[:].indirect(offs_sb[:]))
-        for lo, hi in ((0, 64), (64, 96), (96, 100)):
-            nc.sync.dma_start(x_plane[1][lo:hi, :].bitcast(I32), x_plane[0][4 + lo : 4 + hi, :].bitcast(I32))
+        x_codes = [sbuf([P, S], U16, "x_codes%d" % z) for z in range(PASSES)]
+        for z in range(PASSES):
+            nc.vector.tensor_copy(x_codes[z][:], word_table[z][:].indirect(offs_sb[:]))
+        nc.vector.tensor_copy(x_plane[0][:], scale_table[:, :T].indirect(offs_sb[:]))
 
         operand = {}
 
@@ -139,30 +136,40 @@ def tile_picked_gmem_tanh_p_kernel(
             nc.vector.quantize_mx(out=codes[:].bitcast(FP8X4), scales=plane[:], in_=grouped[:])
             operand[kind, z, b] = (codes[:], plane[:])
 
-        first = [group(nc.scalar.copy, "gate", 0, b) for b in range(BLOCKS)]
-        quantise_block(first[0], "gate", 0, 0, "scale_table")
-        quantise_block(first[1], "gate", 0, 1)
-        window = [load_memory(0, "grouped_gate00")]
-        x_codes.append(sbuf([P, S], U16, "x_codes1", "grouped_gate01"))
-        nc.vector.tensor_copy(x_codes[1][:], word_table[1][:].indirect(offs_sb[:]))
-        window.append(load_memory(1, "warm_in"))
-
-        quantise_pass([nc.scalar.copy, nc.scalar.copy], "cand", 0)
-        second = [group(nc.scalar.copy, "gate", 1, 0), group(nc.scalar.copy, "gate", 1, 1)]
+        by_block = [sbuf([P, PASSES * P * PACK], BF16, "grouped_gate_block%d" % b) for b in range(BLOCKS)]
+        for z in range(PASSES):
+            for b in range(BLOCKS):
+                part = by_block[b][:, z * P * PACK : (z + 1) * P * PACK]
+                interleave(nc.scalar.copy, raw["gate", z][:, :, b * P : (b + 1) * P], part, 0, P)
+        window = []
         for b in range(BLOCKS):
-            quantise_block(second[b], "gate", 1, b)
+            window.append(shared.tile([P, U], F32, name="window%d" % b, offset=4 * U * b, align_bytes=64))
+            nc.sync.dma_start(window[b][:], mem[b * P : (b + 1) * P, :])
+        x_plane.append(sbuf([P, S], U8, "x_plane1"))
+        nc.vector.tensor_copy(x_plane[1][:], scale_table[:, T:].indirect(offs_sb[:]))
+        for b in range(BLOCKS):
+            codes, plane = mx_tiles("gate_block%d" % b)
+            quantise(by_block[b], (codes, plane), 0, N)
+            for z in range(PASSES):
+                operand["gate", z, b] = (codes[:, z * P : (z + 1) * P], plane[:, z * P : (z + 1) * P])
 
-        stay = [sbuf([P, S], F32, "stay%d" % b) for b in range(BLOCKS)]
+        gates = sbuf([P, BLOCKS * S], F32, "stay", "warm_out")
+        stay = [gates[:, b * S : (b + 1) * S] for b in range(BLOCKS)]
         neg_cand = [sbuf([P, S], F32, "neg_cand%d" % b) for b in range(BLOCKS)]
-        for b in range(BLOCKS):
-            product("gate", b, [operand["gate", z, b] for z in range(PASSES)], ACT.Sigmoid, stay[b])
-        last = [group(nc.vector.tensor_copy, "cand", 1, b) for b in range(BLOCKS)]
-        quantise_block(last[0], "cand", 1, 0, "codes_gate10")
-        quantise_block(last[1], "cand", 1, 1, "plane_gate10")
-        for b in range(BLOCKS):
-            product("cand", b, [operand["cand", z, b] for z in range(PASSES)], ACT.Tanh, neg_cand[b])
+        wide = [sbuf([P, N * PACK], BF16, "grouped_cand%d" % z) for z in range(PASSES)]
+        for z, copies in enumerate(((nc.scalar.copy, nc.scalar.copy), (nc.scalar.copy, nc.vector.tensor_copy))):
+            for b in range(BLOCKS):
+                interleave(copies[b], raw["cand", z], wide[z], b * P, (b + 1) * P)
+        for z in range(PASSES):
+            codes, plane = mx_tiles("cand%d" % z)
+            quantise(wide[z], (codes, plane), 0, N)
+            for b in range(BLOCKS):
+                operand["cand", z, b] = (codes[:, b * P : (b + 1) * P], plane[:, b * P : (b + 1) * P])
+        for kind, func, result in (("gate", ACT.Sigmoid, stay), ("cand", ACT.Tanh, neg_cand)):
+            for b in range(BLOCKS):
+                product(kind, b, [operand[kind, z, b] for z in range(PASSES)], func, result[b])
 
-        kept = [sbuf([P, S], F32, "kept%d" % b) for b in range(BLOCKS)]
+        kept = [sbuf([P, S], F32, "kept%d" % b, "grouped_cand%d" % (1 - b)) for b in range(BLOCKS)]
         fresh = [sbuf([P, S], F32, "fresh%d" % b) for b in range(BLOCKS)]
         for b in range(BLOCKS):
             nc.vector.tensor_tensor(kept[b][:], window[b][:].indirect(slot_sb[:]), stay[b][:], ALU.mult)

@@ -87,8 +87,9 @@ def tile_picked_gmem_tanh_p_kernel(
         scale_table = sbuf([P, PASSES * T], U8, "scale_table")
         nc.vector.memset(scale_table[:].bitcast(I32), 0)
         x_plane = [sbuf([P, S], U8, "x_plane0")]
-        warm_in = sbuf([P, 1], F32, "warm_in")
-        warm_out = sbuf([P, 1], F32, "warm_out")
+        warm_in = sbuf([P, 32], F32, "warm_in")
+        late = ctx.enter_context(tc.tile_pool(name="late", bufs=1))
+        warm_out = late.tile([P, 32], F32, name="warm_out", offset=4 * U - 64, align_bytes=64)
         nc.vector.memset(warm_in[:], 0.0)
         nc.scalar.activation(out=warm_out[:], in_=warm_in[:], func=ACT.Sigmoid)
 
@@ -104,10 +105,12 @@ def tile_picked_gmem_tanh_p_kernel(
                 scale_table[QUAD * q : QUAD * q + 4, :].bitcast(I32).rearrange("r (z c) -> r z c", z=PASSES),
                 x_scales[:, 4 * q : 4 * q + 4, :].bitcast(I32).rearrange("z r c -> r z c"),
             )
-        raw_next = sbuf([P, 3, PACK, N], F32, "raw_next", "warm_out")
-        for i, (kind, w, z) in enumerate((("gate", w2, 1), ("cand", w1, 0), ("cand", w1, 1))):
-            raw[kind, z] = raw_next[:, i, :, :]
-            nc.sync.dma_start(raw[kind, z], w[z * K_PASS : (z + 1) * K_PASS, :].rearrange("(p j) c -> p j c", j=PACK))
+        raw["gate", 1] = load_weights(w2, 1, "raw_gate1", "warm_in")
+        for z in range(PASSES):
+            raw["cand", z] = late.tile([P, PACK, N], F32, name="raw_cand%d" % z, offset=4 * U * z, align_bytes=64)
+            nc.sync.dma_start(
+                raw["cand", z][:], w1[z * K_PASS : (z + 1) * K_PASS, :].rearrange("(p j) c -> p j c", j=PACK)
+            )
 
         x_codes = [sbuf([P, S], U16, "x_codes%d" % z) for z in range(PASSES)]
         for z in range(PASSES):
@@ -136,30 +139,30 @@ def tile_picked_gmem_tanh_p_kernel(
             nc.vector.quantize_mx(out=codes[:].bitcast(FP8X4), scales=plane[:], in_=grouped[:])
             operand[kind, z, b] = (codes[:], plane[:])
 
-        by_block = [sbuf([P, PASSES * P * PACK], BF16, "grouped_gate_block%d" % b) for b in range(BLOCKS)]
+        second = sbuf([P, PASSES * P * PACK], BF16, "grouped_gate_second")
+        first = []
         for z in range(PASSES):
-            for b in range(BLOCKS):
-                part = by_block[b][:, z * P * PACK : (z + 1) * P * PACK]
-                interleave(nc.scalar.copy, raw["gate", z][:, :, b * P : (b + 1) * P], part, 0, P)
+            first.append(group(nc.scalar.copy, "gate", z, 0))
+            interleave(nc.scalar.copy, raw["gate", z][:, :, P:], second[:, z * P * PACK : (z + 1) * P * PACK], 0, P)
+        quantise_block(first[0], "gate", 0, 0)
         window = []
         for b in range(BLOCKS):
             window.append(shared.tile([P, U], F32, name="window%d" % b, offset=4 * U * b, align_bytes=64))
             nc.sync.dma_start(window[b][:], mem[b * P : (b + 1) * P, :])
         x_plane.append(sbuf([P, S], U8, "x_plane1"))
         nc.vector.tensor_copy(x_plane[1][:], scale_table[:, T:].indirect(offs_sb[:]))
-        for b in range(BLOCKS):
-            codes, plane = mx_tiles("gate_block%d" % b)
-            quantise(by_block[b], (codes, plane), 0, N)
-            for z in range(PASSES):
-                operand["gate", z, b] = (codes[:, z * P : (z + 1) * P], plane[:, z * P : (z + 1) * P])
+        quantise_block(first[1], "gate", 1, 0)
+        codes, plane = mx_tiles("gate_second")
+        quantise(second, (codes, plane), 0, N)
+        for z in range(PASSES):
+            operand["gate", z, 1] = (codes[:, z * P : (z + 1) * P], plane[:, z * P : (z + 1) * P])
 
-        gates = sbuf([P, BLOCKS * S], F32, "stay", "warm_out")
-        stay = [gates[:, b * S : (b + 1) * S] for b in range(BLOCKS)]
+        stay = [late.tile([P, S], F32, name="stay%d" % b, offset=4 * S * b, align_bytes=64) for b in range(BLOCKS)]
         neg_cand = [sbuf([P, S], F32, "neg_cand%d" % b) for b in range(BLOCKS)]
         wide = [sbuf([P, N * PACK], BF16, "grouped_cand%d" % z) for z in range(PASSES)]
-        for z, copies in enumerate(((nc.scalar.copy, nc.scalar.copy), (nc.scalar.copy, nc.vector.tensor_copy))):
-            for b in range(BLOCKS):
-                interleave(copies[b], raw["cand", z], wide[z], b * P, (b + 1) * P)
+        for b in range(BLOCKS):
+            interleave(nc.scalar.copy, raw["cand", 0], wide[0], b * P, (b + 1) * P)
+        interleave(nc.vector.tensor_copy, raw["cand", 1], wide[1], 0, N)
         for z in range(PASSES):
             codes, plane = mx_tiles("cand%d" % z)
             quantise(wide[z], (codes, plane), 0, N)
@@ -169,7 +172,7 @@ def tile_picked_gmem_tanh_p_kernel(
             for b in range(BLOCKS):
                 product(kind, b, [operand[kind, z, b] for z in range(PASSES)], func, result[b])
 
-        kept = [sbuf([P, S], F32, "kept%d" % b, "grouped_cand%d" % (1 - b)) for b in range(BLOCKS)]
+        kept = [sbuf([P, S], F32, "kept%d" % b) for b in range(BLOCKS)]
         fresh = [sbuf([P, S], F32, "fresh%d" % b) for b in range(BLOCKS)]
         for b in range(BLOCKS):
             nc.vector.tensor_tensor(kept[b][:], window[b][:].indirect(slot_sb[:]), stay[b][:], ALU.mult)

@@ -22,7 +22,10 @@ K_PASS = P * PACK
 PASSES = K // K_PASS
 BLOCKS = N // P
 QUAD = 32
+SCALE_ROWS = 4
 RUN = 4
+LIST_ROWS = 16
+ROW_BYTES = 4 * U
 
 
 def tile_picked_gmem_tanh_p_kernel(
@@ -32,46 +35,94 @@ def tile_picked_gmem_tanh_p_kernel(
     with ExitStack() as ctx:
         lists = ctx.enter_context(tc.tile_pool(name="lists", bufs=1))
         keep = ctx.enter_context(tc.tile_pool(name="keep", bufs=1))
+        placed = ctx.enter_context(tc.tile_pool(name="placed", bufs=1))
         psum = ctx.enter_context(tc.psum_pool(name="psum", bufs=1))
 
-        offs_sb = lists.tile([P, S // 16], U16, name="offs_sb")
-        slot_sb = lists.tile([P, S // 16], U16, name="slot_sb")
+        def sbuf(shape, dtype, name, buffer_of=None):
+            return keep.tile(shape, dtype, name=name, tag=buffer_of or name, align_bytes=64)
 
-        def sbuf(shape, dtype, name, after=None):
-            return keep.tile(shape, dtype, name=name, tag=after or name, align_bytes=64)
+        def load_weights(raw, w, z):
+            nc.sync.dma_start(raw, w[z * K_PASS : (z + 1) * K_PASS, :].rearrange("(p t) m -> p t m", t=PACK))
 
-        def load_words(z, after=None):
-            table = sbuf([P, T], U16, "word_table%d" % z, after)
-            nc.sync.dma_start(table[:].bitcast(I32), x_words[z].bitcast(I32))
-            return table
-
-        def load_weights(w, z, name, after=None):
-            raw = sbuf([P, PACK, N], F32, name, after)
-            nc.sync.dma_start(raw[:], w[z * K_PASS : (z + 1) * K_PASS, :].rearrange("(p j) c -> p j c", j=PACK))
-            return raw
-
-        def load_memory(b, after=None):
-            window = sbuf([P, U], F32, "window%d" % b, after)
-            nc.sync.dma_start(window[:], mem[b * P : (b + 1) * P, :])
-            return window
-
-        def interleave(engine_copy, raw, grouped, lo, hi):
+        def interleave(engine_copy, grouped, raw):
             engine_copy(
-                out=grouped[:, lo * PACK : hi * PACK].rearrange("p (c i j) -> p c j i", i=RUN, j=PACK),
-                in_=raw[:, :, lo:hi].rearrange("p j (c i) -> p c j i", i=RUN),
+                out=grouped.rearrange("p (c i t) -> p c t i", i=RUN, t=PACK),
+                in_=raw.rearrange("p t (c i) -> p c t i", i=RUN),
             )
 
-        def quantise(grouped, operand, lo, hi):
-            codes, plane = operand
-            nc.vector.quantize_mx(
-                out=codes[:, lo:hi].bitcast(FP8X4), scales=plane[:, lo:hi], in_=grouped[:, lo * PACK : hi * PACK]
+        def quantise(name, grouped):
+            width = grouped.shape[1] // PACK
+            codes = sbuf([P, width], U32, "codes_" + name)
+            plane = sbuf([P, width], U8, "plane_" + name)
+            nc.vector.quantize_mx(out=codes[:].bitcast(FP8X4), scales=plane[:], in_=grouped[:])
+            return [(codes[:, lo : lo + P], plane[:, lo : lo + P]) for lo in range(0, width, P)]
+
+        def rows_of(b):
+            return slice(b * P, (b + 1) * P)
+
+        def grouped_part(i):
+            return slice(i * P * PACK, (i + 1) * P * PACK)
+
+        scale_table = sbuf([P, PASSES * T], U8, "scale_table")
+        nc.vector.memset(scale_table[:].bitcast(I32), 0)
+
+        warm_in = sbuf([P, 1], F32, "warm_in")
+        warm_out = sbuf([P, 1], F32, "warm_out")
+        nc.vector.memset(warm_in[:], 0.0)
+        nc.scalar.activation(out=warm_out[:], in_=warm_in[:], func=ACT.Sigmoid)
+
+        offs_sb = lists.tile([P, S // LIST_ROWS], U16, name="offs_sb")
+        slot_sb = lists.tile([P, S // LIST_ROWS], U16, name="slot_sb")
+        word_table = [sbuf([P, T], U16, "word_table%d" % z) for z in range(PASSES)]
+        nc.sync.dma_start(offs_sb[:], offs)
+        for z in range(PASSES):
+            nc.sync.dma_start(word_table[z][:].bitcast(I32), x_words[z].bitcast(I32))
+        raw_first = placed.tile([P, PACK, N], F32, name="raw_first", offset=ROW_BYTES // 2, align_bytes=64)
+        load_weights(raw_first[:], w2, 0)
+        nc.sync.dma_start(slot_sb[:], slot)
+        for q in range(P // QUAD):
+            nc.sync.dma_start(
+                scale_table[QUAD * q : QUAD * q + SCALE_ROWS, :].bitcast(I32).rearrange("r (z c) -> r z c", z=PASSES),
+                x_scales[:, SCALE_ROWS * q : SCALE_ROWS * (q + 1), :].bitcast(I32).rearrange("z r c -> r z c"),
             )
+        raw_later = sbuf([P, 1 + PASSES, PACK, N], F32, "raw_later", "warm_in")
+        raw_gate = [raw_first[:], raw_later[:, 0, :, :]]
+        raw_cand = [raw_later[:, 1 + z, :, :] for z in range(PASSES)]
+        load_weights(raw_gate[1], w2, 1)
+        for z in range(PASSES):
+            load_weights(raw_cand[z], w1, z)
 
-        def mx_tiles(name, after=None):
-            return sbuf([P, N], U32, "codes_" + name, after), sbuf([P, N], U8, "plane_" + name)
+        x_codes = [sbuf([P, S], U16, "x_codes%d" % z) for z in range(PASSES)]
+        x_plane = [sbuf([P, S], U8, "x_plane%d" % z) for z in range(PASSES)]
+        for z in range(PASSES):
+            nc.vector.tensor_copy(x_codes[z][:], word_table[z][:].indirect(offs_sb[:]))
+        nc.vector.tensor_copy(x_plane[0][:], scale_table[:, :T].indirect(offs_sb[:]))
 
-        def product(kind, b, operands, func, result):
-            acc = psum.tile([P, S], F32, name="acc_%s%d" % (kind, b))
+        grouped_gate0 = [sbuf([P, P * PACK], BF16, "grouped_gate0_pass%d" % z) for z in range(PASSES)]
+        grouped_gate1 = sbuf([P, PASSES * P * PACK], BF16, "grouped_gate1")
+        for z in range(PASSES):
+            interleave(nc.scalar.copy, grouped_gate0[z][:], raw_gate[z][:, :, rows_of(0)])
+            interleave(nc.scalar.copy, grouped_gate1[:, grouped_part(z)], raw_gate[z][:, :, rows_of(1)])
+        gate0 = quantise("gate0_pass0", grouped_gate0[0])
+
+        window = []
+        for b in range(BLOCKS):
+            window.append(placed.tile([P, U], F32, name="window%d" % b, offset=ROW_BYTES * b, align_bytes=64))
+            nc.sync.dma_start(window[b][:], mem[rows_of(b), :])
+
+        nc.vector.tensor_copy(x_plane[1][:], scale_table[:, T:].indirect(offs_sb[:]))
+        gate0 = gate0 + quantise("gate0_pass1", grouped_gate0[1])
+        gate = [gate0, quantise("gate1", grouped_gate1)]
+
+        grouped_cand = [sbuf([P, N * PACK], BF16, "grouped_cand%d" % z) for z in range(PASSES)]
+        for b in range(BLOCKS):
+            interleave(nc.scalar.copy, grouped_cand[0][:, grouped_part(b)], raw_cand[0][:, :, rows_of(b)])
+        interleave(nc.vector.tensor_copy, grouped_cand[1][:], raw_cand[1])
+        cand_by_pass = [quantise("cand%d" % z, grouped_cand[z]) for z in range(PASSES)]
+        cand = [[cand_by_pass[z][b] for z in range(PASSES)] for b in range(BLOCKS)]
+
+        def product(name, operands, func, result):
+            acc = psum.tile([P, S], F32, name="acc_" + name)
             for z, (codes, plane) in enumerate(operands):
                 nc.tensor.matmul_mx(
                     out=acc[:],
@@ -84,93 +135,12 @@ def tile_picked_gmem_tanh_p_kernel(
                 )
             nc.scalar.activation(out=result[:], in_=acc[:], func=func, scale=-1.0)
 
-        scale_table = sbuf([P, PASSES * T], U8, "scale_table")
-        nc.vector.memset(scale_table[:].bitcast(I32), 0)
-        x_plane = [sbuf([P, S], U8, "x_plane0")]
-        warm_in = sbuf([P, 32], F32, "warm_in")
-        late = ctx.enter_context(tc.tile_pool(name="late", bufs=1))
-        warm_out = late.tile([P, 32], F32, name="warm_out", offset=4 * U - 64, align_bytes=64)
-        nc.vector.memset(warm_in[:], 0.0)
-        nc.scalar.activation(out=warm_out[:], in_=warm_in[:], func=ACT.Sigmoid)
-
-        nc.sync.dma_start(offs_sb[:], offs)
-        word_table = [load_words(z) for z in range(PASSES)]
-        shared = ctx.enter_context(tc.tile_pool(name="shared", bufs=1))
-        raw_first = shared.tile([P, PACK, N], F32, name="raw_gate0", offset=2 * U, align_bytes=64)
-        nc.sync.dma_start(raw_first[:], w2[:K_PASS, :].rearrange("(p j) c -> p j c", j=PACK))
-        raw = {("gate", 0): raw_first}
-        nc.sync.dma_start(slot_sb[:], slot)
-        for q in range(P // QUAD):
-            nc.sync.dma_start(
-                scale_table[QUAD * q : QUAD * q + 4, :].bitcast(I32).rearrange("r (z c) -> r z c", z=PASSES),
-                x_scales[:, 4 * q : 4 * q + 4, :].bitcast(I32).rearrange("z r c -> r z c"),
-            )
-        raw["gate", 1] = load_weights(w2, 1, "raw_gate1", "warm_in")
-        for z in range(PASSES):
-            raw["cand", z] = late.tile([P, PACK, N], F32, name="raw_cand%d" % z, offset=4 * U * z, align_bytes=64)
-            nc.sync.dma_start(
-                raw["cand", z][:], w1[z * K_PASS : (z + 1) * K_PASS, :].rearrange("(p j) c -> p j c", j=PACK)
-            )
-
-        x_codes = [sbuf([P, S], U16, "x_codes%d" % z) for z in range(PASSES)]
-        for z in range(PASSES):
-            nc.vector.tensor_copy(x_codes[z][:], word_table[z][:].indirect(offs_sb[:]))
-        nc.vector.tensor_copy(x_plane[0][:], scale_table[:, :T].indirect(offs_sb[:]))
-
-        operand = {}
-
-        def group(engine_copy, kind, z, b):
-            grouped = sbuf([P, P * PACK], BF16, "grouped_%s%d%d" % (kind, z, b))
-            interleave(engine_copy, raw[kind, z][:, :, b * P : (b + 1) * P], grouped, 0, P)
-            return grouped
-
-        def quantise_pass(copies, kind, z):
-            grouped = sbuf([P, N * PACK], BF16, "grouped_%s%d" % (kind, z))
-            for b in range(BLOCKS):
-                interleave(copies[b], raw[kind, z], grouped, b * P, (b + 1) * P)
-            codes, plane = mx_tiles("%s%d" % (kind, z))
-            quantise(grouped, (codes, plane), 0, N)
-            for b in range(BLOCKS):
-                operand[kind, z, b] = (codes[:, b * P : (b + 1) * P], plane[:, b * P : (b + 1) * P])
-
-        def quantise_block(grouped, kind, z, b, after=None):
-            codes = sbuf([P, P], U32, "codes_%s%d%d" % (kind, z, b), after)
-            plane = sbuf([P, P], U8, "plane_%s%d%d" % (kind, z, b))
-            nc.vector.quantize_mx(out=codes[:].bitcast(FP8X4), scales=plane[:], in_=grouped[:])
-            operand[kind, z, b] = (codes[:], plane[:])
-
-        second = sbuf([P, PASSES * P * PACK], BF16, "grouped_gate_second")
-        first = []
-        for z in range(PASSES):
-            first.append(group(nc.scalar.copy, "gate", z, 0))
-            interleave(nc.scalar.copy, raw["gate", z][:, :, P:], second[:, z * P * PACK : (z + 1) * P * PACK], 0, P)
-        quantise_block(first[0], "gate", 0, 0)
-        window = []
-        for b in range(BLOCKS):
-            window.append(shared.tile([P, U], F32, name="window%d" % b, offset=4 * U * b, align_bytes=64))
-            nc.sync.dma_start(window[b][:], mem[b * P : (b + 1) * P, :])
-        x_plane.append(sbuf([P, S], U8, "x_plane1"))
-        nc.vector.tensor_copy(x_plane[1][:], scale_table[:, T:].indirect(offs_sb[:]))
-        quantise_block(first[1], "gate", 1, 0)
-        codes, plane = mx_tiles("gate_second")
-        quantise(second, (codes, plane), 0, N)
-        for z in range(PASSES):
-            operand["gate", z, 1] = (codes[:, z * P : (z + 1) * P], plane[:, z * P : (z + 1) * P])
-
-        stay = [late.tile([P, S], F32, name="stay%d" % b, offset=4 * S * b, align_bytes=64) for b in range(BLOCKS)]
+        stay = [sbuf([P, S], F32, "stay0", "grouped_gate1"), sbuf([P, S], F32, "stay1")]
         neg_cand = [sbuf([P, S], F32, "neg_cand%d" % b) for b in range(BLOCKS)]
-        wide = [sbuf([P, N * PACK], BF16, "grouped_cand%d" % z) for z in range(PASSES)]
         for b in range(BLOCKS):
-            interleave(nc.scalar.copy, raw["cand", 0], wide[0], b * P, (b + 1) * P)
-        interleave(nc.vector.tensor_copy, raw["cand", 1], wide[1], 0, N)
-        for z in range(PASSES):
-            codes, plane = mx_tiles("cand%d" % z)
-            quantise(wide[z], (codes, plane), 0, N)
-            for b in range(BLOCKS):
-                operand["cand", z, b] = (codes[:, b * P : (b + 1) * P], plane[:, b * P : (b + 1) * P])
-        for kind, func, result in (("gate", ACT.Sigmoid, stay), ("cand", ACT.Tanh, neg_cand)):
-            for b in range(BLOCKS):
-                product(kind, b, [operand[kind, z, b] for z in range(PASSES)], func, result[b])
+            product("gate%d" % b, gate[b], ACT.Sigmoid, stay[b])
+        for b in range(BLOCKS):
+            product("cand%d" % b, cand[b], ACT.Tanh, neg_cand[b])
 
         kept = [sbuf([P, S], F32, "kept%d" % b) for b in range(BLOCKS)]
         fresh = [sbuf([P, S], F32, "fresh%d" % b) for b in range(BLOCKS)]
@@ -182,4 +152,4 @@ def tile_picked_gmem_tanh_p_kernel(
             )
         for b in range(BLOCKS):
             nc.vector.tensor_tensor(window[b][:].indirect(slot_sb[:]), kept[b][:], fresh[b][:], ALU.add)
-            nc.sync.dma_start(out[b * P : (b + 1) * P, :], window[b][:])
+            nc.sync.dma_start(out[rows_of(b), :], window[b][:])

@@ -25,6 +25,7 @@ QUAD = 32
 SCALE_ROWS = 4
 RUN = 4
 LIST_ROWS = 16
+HALF = S // 2
 ROW_BYTES = 4 * U
 
 
@@ -144,12 +145,24 @@ def tile_picked_gmem_tanh_p_kernel(
 
         kept = [sbuf([P, S], F32, "kept%d" % b) for b in range(BLOCKS)]
         fresh = [sbuf([P, S], F32, "fresh%d" % b) for b in range(BLOCKS)]
-        for b in range(BLOCKS):
-            nc.vector.tensor_tensor(kept[b][:], window[b][:].indirect(slot_sb[:]), stay[b][:], ALU.mult)
-        for b in range(BLOCKS):
+        old1 = sbuf([P, S], F32, "old1")
+        new0 = [sbuf([P, HALF], F32, "new0_%d" % h) for h in range(2)]
+
+        def gate_times_candidate(b):
             nc.vector.scalar_tensor_tensor(
                 out=fresh[b][:], in0=stay[b][:], scalar=1.0, in1=neg_cand[b][:], op0=ALU.subtract, op1=ALU.mult
             )
-        for b in range(BLOCKS):
-            nc.vector.tensor_tensor(window[b][:].indirect(slot_sb[:]), kept[b][:], fresh[b][:], ALU.add)
-            nc.sync.dma_start(out[rows_of(b), :], window[b][:])
+
+        nc.vector.tensor_tensor(kept[0][:], window[0][:].indirect(slot_sb[:]), stay[0][:], ALU.mult)
+        nc.scalar.activation(out=old1[:], in_=window[1][:].indirect(slot_sb[:]), func=ACT.Copy)
+        gate_times_candidate(0)
+        nc.vector.tensor_tensor(kept[1][:], old1[:], stay[1][:], ALU.mult)
+        for h in range(2):
+            cols = slice(h * HALF, (h + 1) * HALF)
+            offsets = slot_sb[:, h * HALF // LIST_ROWS : (h + 1) * HALF // LIST_ROWS]
+            nc.vector.tensor_tensor(new0[h][:], kept[0][:, cols], fresh[0][:, cols], ALU.add)
+            nc.scalar.activation(out=window[0][:].indirect(offsets), in_=new0[h][:], func=ACT.Copy)
+        nc.sync.dma_start(out[rows_of(0), :], window[0][:])
+        gate_times_candidate(1)
+        nc.vector.tensor_tensor(window[1][:].indirect(slot_sb[:]), kept[1][:], fresh[1][:], ALU.add)
+        nc.sync.dma_start(out[rows_of(1), :], window[1][:])

@@ -64,6 +64,9 @@ def tile_picked_gmem_tanh_p_kernel(
         def grouped_part(i):
             return slice(i * P * PACK, (i + 1) * P * PACK)
 
+        def over(raw_index, shape, dtype, name, at=0):
+            return placed.tile(shape, dtype, name=name, offset=raw_index * ROW_BYTES + at, align_bytes=64)
+
         scale_table = sbuf([P, PASSES * T], U8, "scale_table")
         nc.vector.memset(scale_table[:].bitcast(I32), 0)
 
@@ -75,55 +78,57 @@ def tile_picked_gmem_tanh_p_kernel(
         offs_sb = lists.tile([P, S // LIST_ROWS], U16, name="offs_sb")
         slot_sb = lists.tile([P, S // LIST_ROWS], U16, name="slot_sb")
         word_table = [sbuf([P, T], U16, "word_table%d" % z) for z in range(PASSES)]
-        nc.sync.dma_start(offs_sb[:], offs)
-        for z in range(PASSES):
+        sources = [(w2, 0), (w2, 1), (w1, 0), (w1, 1)]
+        raw = [over(i, [P, PACK, N], F32, "raw%d" % i) for i in range(len(sources))]
+        window = [sbuf([P, U], F32, "window%d" % b) for b in range(BLOCKS)]
+
+        def load_words(z):
             nc.sync.dma_start(word_table[z][:].bitcast(I32), x_words[z].bitcast(I32))
-        raw_first = placed.tile([P, PACK, N], F32, name="raw_first", offset=ROW_BYTES // 2, align_bytes=64)
-        load_weights(raw_first[:], w2, 0)
-        nc.sync.dma_start(slot_sb[:], slot)
+
+        nc.sync.dma_start(offs_sb[:], offs)
+        load_words(0)
+        load_words(1)
         for q in range(P // QUAD):
             nc.sync.dma_start(
                 scale_table[QUAD * q : QUAD * q + SCALE_ROWS, :].bitcast(I32).rearrange("r (z c) -> r z c", z=PASSES),
                 x_scales[:, SCALE_ROWS * q : SCALE_ROWS * (q + 1), :].bitcast(I32).rearrange("z r c -> r z c"),
             )
-        raw_later = sbuf([P, 1 + PASSES, PACK, N], F32, "raw_later", "warm_in")
-        raw_gate = [raw_first[:], raw_later[:, 0, :, :]]
-        raw_cand = [raw_later[:, 1 + z, :, :] for z in range(PASSES)]
-        load_weights(raw_gate[1], w2, 1)
-        for z in range(PASSES):
-            load_weights(raw_cand[z], w1, z)
+        load_weights(raw[0][:], *sources[0])
+        nc.sync.dma_start(slot_sb[:], slot)
+        for i in range(1, len(sources)):
+            load_weights(raw[i][:], *sources[i])
+        for b in range(BLOCKS):
+            nc.sync.dma_start(window[b][:], mem[rows_of(b), :])
+
+        def interleave_on_scalar(i):
+            grouped = sbuf([P, N * PACK], BF16, "grouped%d" % i)
+            for b in range(BLOCKS):
+                interleave(nc.scalar.copy, grouped[:, grouped_part(b)], raw[i][:, :, rows_of(b)])
+            return grouped
 
         x_codes = [sbuf([P, S], U16, "x_codes%d" % z) for z in range(PASSES)]
-        x_plane = [sbuf([P, S], U8, "x_plane%d" % z) for z in range(PASSES)]
+        x_plane = [sbuf([P, S], U8, "x_plane0"), over(0, [P, S], U8, "x_plane1")]
         for z in range(PASSES):
             nc.vector.tensor_copy(x_codes[z][:], word_table[z][:].indirect(offs_sb[:]))
         nc.vector.tensor_copy(x_plane[0][:], scale_table[:, :T].indirect(offs_sb[:]))
-
-        grouped_gate0 = [sbuf([P, P * PACK], BF16, "grouped_gate0_pass%d" % z) for z in range(PASSES)]
-        grouped_gate1 = sbuf([P, PASSES * P * PACK], BF16, "grouped_gate1")
-        for z in range(PASSES):
-            interleave(nc.scalar.copy, grouped_gate0[z][:], raw_gate[z][:, :, rows_of(0)])
-            interleave(nc.scalar.copy, grouped_gate1[:, grouped_part(z)], raw_gate[z][:, :, rows_of(1)])
-        gate0 = quantise("gate0_pass0", grouped_gate0[0])
-
-        window = []
+        grouped_first = [sbuf([P, P * PACK], BF16, "grouped_first%d" % b) for b in range(BLOCKS)]
         for b in range(BLOCKS):
-            window.append(placed.tile([P, U], F32, name="window%d" % b, offset=ROW_BYTES * b, align_bytes=64))
-            nc.sync.dma_start(window[b][:], mem[rows_of(b), :])
-
+            interleave(nc.scalar.copy, grouped_first[b][:], raw[0][:, :, rows_of(b)])
+        gate_first = [quantise("gate%d_pass0" % b, grouped_first[b])[0] for b in range(BLOCKS)]
         nc.vector.tensor_copy(x_plane[1][:], scale_table[:, T:].indirect(offs_sb[:]))
-        gate0 = gate0 + quantise("gate0_pass1", grouped_gate0[1])
-        gate = [gate0, quantise("gate1", grouped_gate1)]
+        gate_second = quantise("gate_pass1", interleave_on_scalar(1))
+        grouped_cand0 = [sbuf([P, P * PACK], BF16, "grouped_cand0_pass%d" % z) for z in range(PASSES)]
+        grouped_cand1 = sbuf([P, PASSES * P * PACK], BF16, "grouped_cand1")
+        interleave(nc.scalar.copy, grouped_cand0[0][:], raw[2][:, :, rows_of(0)])
+        interleave(nc.scalar.copy, grouped_cand1[:, grouped_part(0)], raw[2][:, :, rows_of(1)])
+        interleave(nc.scalar.copy, grouped_cand0[1][:], raw[3][:, :, rows_of(0)])
+        interleave(nc.vector.tensor_copy, grouped_cand1[:, grouped_part(1)], raw[3][:, :, rows_of(1)])
+        gate = [[gate_first[b], gate_second[b]] for b in range(BLOCKS)]
+        cand0 = [quantise("cand0_pass%d" % z, grouped_cand0[z])[0] for z in range(PASSES)]
+        cand = [cand0, quantise("cand1", grouped_cand1)]
 
-        grouped_cand = [sbuf([P, N * PACK], BF16, "grouped_cand%d" % z) for z in range(PASSES)]
-        for b in range(BLOCKS):
-            interleave(nc.scalar.copy, grouped_cand[0][:, grouped_part(b)], raw_cand[0][:, :, rows_of(b)])
-        interleave(nc.vector.tensor_copy, grouped_cand[1][:], raw_cand[1])
-        cand_by_pass = [quantise("cand%d" % z, grouped_cand[z]) for z in range(PASSES)]
-        cand = [[cand_by_pass[z][b] for z in range(PASSES)] for b in range(BLOCKS)]
-
-        def product(name, operands, func, result):
-            acc = psum.tile([P, S], F32, name="acc_" + name)
+        def product(name, bank, operands, func, result):
+            acc = psum.tile([P, S], F32, name="acc_" + name, tag="bank%d" % bank)
             for z, (codes, plane) in enumerate(operands):
                 nc.tensor.matmul_mx(
                     out=acc[:],
@@ -136,12 +141,12 @@ def tile_picked_gmem_tanh_p_kernel(
                 )
             nc.scalar.activation(out=result[:], in_=acc[:], func=func, scale=-1.0)
 
-        stay = [sbuf([P, S], F32, "stay0", "grouped_gate1"), sbuf([P, S], F32, "stay1")]
+        stay = [over(3, [P, S], F32, "stay%d" % b, at=4 * S * b) for b in range(BLOCKS)]
         neg_cand = [sbuf([P, S], F32, "neg_cand%d" % b) for b in range(BLOCKS)]
         for b in range(BLOCKS):
-            product("gate%d" % b, gate[b], ACT.Sigmoid, stay[b])
+            product("gate%d" % b, b, gate[b], ACT.Sigmoid, stay[b])
         for b in range(BLOCKS):
-            product("cand%d" % b, cand[b], ACT.Tanh, neg_cand[b])
+            product("cand%d" % b, 2 - 2 * b, cand[b], ACT.Tanh, neg_cand[b])
 
         kept = [sbuf([P, S], F32, "kept%d" % b) for b in range(BLOCKS)]
         fresh = [sbuf([P, S], F32, "fresh%d" % b) for b in range(BLOCKS)]
@@ -153,16 +158,19 @@ def tile_picked_gmem_tanh_p_kernel(
                 out=fresh[b][:], in0=stay[b][:], scalar=1.0, in1=neg_cand[b][:], op0=ALU.subtract, op1=ALU.mult
             )
 
-        nc.vector.tensor_tensor(kept[0][:], window[0][:].indirect(slot_sb[:]), stay[0][:], ALU.mult)
-        nc.scalar.activation(out=old1[:], in_=window[1][:].indirect(slot_sb[:]), func=ACT.Copy)
-        gate_times_candidate(0)
-        nc.vector.tensor_tensor(kept[1][:], old1[:], stay[1][:], ALU.mult)
-        for h in range(2):
+        def scatter_half(h):
             cols = slice(h * HALF, (h + 1) * HALF)
             offsets = slot_sb[:, h * HALF // LIST_ROWS : (h + 1) * HALF // LIST_ROWS]
             nc.vector.tensor_tensor(new0[h][:], kept[0][:, cols], fresh[0][:, cols], ALU.add)
             nc.scalar.activation(out=window[0][:].indirect(offsets), in_=new0[h][:], func=ACT.Copy)
-        nc.sync.dma_start(out[rows_of(0), :], window[0][:])
+
+        nc.vector.tensor_tensor(kept[0][:], window[0][:].indirect(slot_sb[:]), stay[0][:], ALU.mult)
+        nc.scalar.activation(out=old1[:], in_=window[1][:].indirect(slot_sb[:]), func=ACT.Copy)
+        gate_times_candidate(0)
         gate_times_candidate(1)
+        scatter_half(0)
+        nc.vector.tensor_tensor(kept[1][:], old1[:], stay[1][:], ALU.mult)
+        scatter_half(1)
+        nc.sync.dma_start(out[rows_of(0), :], window[0][:])
         nc.vector.tensor_tensor(window[1][:].indirect(slot_sb[:]), kept[1][:], fresh[1][:], ALU.add)
         nc.sync.dma_start(out[rows_of(1), :], window[1][:])

@@ -26,6 +26,7 @@ SCALE_ROWS = 4
 RUN = 4
 LIST_ROWS = 16
 HALF = S // 2
+SCALAR_GATHERS = 384
 ROW_BYTES = 4 * U
 
 
@@ -117,15 +118,17 @@ def tile_picked_gmem_tanh_p_kernel(
         gate_first = [quantise("gate%d_pass0" % b, grouped_first[b])[0] for b in range(BLOCKS)]
         nc.vector.tensor_copy(x_plane[1][:], scale_table[:, T:].indirect(offs_sb[:]))
         gate_second = quantise("gate_pass1", interleave_on_scalar(1))
-        grouped_cand0 = [sbuf([P, P * PACK], BF16, "grouped_cand0_pass%d" % z) for z in range(PASSES)]
-        grouped_cand1 = sbuf([P, PASSES * P * PACK], BF16, "grouped_cand1")
-        interleave(nc.scalar.copy, grouped_cand0[0][:], raw[2][:, :, rows_of(0)])
-        interleave(nc.scalar.copy, grouped_cand1[:, grouped_part(0)], raw[2][:, :, rows_of(1)])
-        interleave(nc.scalar.copy, grouped_cand0[1][:], raw[3][:, :, rows_of(0)])
-        interleave(nc.vector.tensor_copy, grouped_cand1[:, grouped_part(1)], raw[3][:, :, rows_of(1)])
+        grouped_cand = [
+            [sbuf([P, P * PACK], BF16, "grouped_cand0_pass0"), over(4, [P, P * PACK], BF16, "grouped_cand1_pass0", at=4 * S - P * PACK)],
+            [sbuf([P, P * PACK], BF16, "grouped_cand%d_pass1" % b) for b in range(BLOCKS)],
+        ]
+        cand_by_pass = []
+        for z, copies in enumerate(((nc.scalar.copy, nc.scalar.copy), (nc.vector.tensor_copy, nc.scalar.copy))):
+            for b in range(BLOCKS):
+                interleave(copies[b], grouped_cand[z][b][:], raw[2 + z][:, :, rows_of(b)])
+            cand_by_pass.append([quantise("cand%d_pass%d" % (b, z), grouped_cand[z][b])[0] for b in range(BLOCKS)])
         gate = [[gate_first[b], gate_second[b]] for b in range(BLOCKS)]
-        cand0 = [quantise("cand0_pass%d" % z, grouped_cand0[z])[0] for z in range(PASSES)]
-        cand = [cand0, quantise("cand1", grouped_cand1)]
+        cand = [[cand_by_pass[z][b] for z in range(PASSES)] for b in range(BLOCKS)]
 
         def product(name, bank, operands, func, result):
             acc = psum.tile([P, S], F32, name="acc_" + name, tag="bank%d" % bank)
@@ -141,36 +144,50 @@ def tile_picked_gmem_tanh_p_kernel(
                 )
             nc.scalar.activation(out=result[:], in_=acc[:], func=func, scale=-1.0)
 
-        stay = [over(3, [P, S], F32, "stay%d" % b, at=4 * S * b) for b in range(BLOCKS)]
+        stay = [over(4, [P, S], F32, "stay%d" % b, at=4 * S * b) for b in range(BLOCKS)]
         neg_cand = [sbuf([P, S], F32, "neg_cand%d" % b) for b in range(BLOCKS)]
         for b in range(BLOCKS):
             product("gate%d" % b, b, gate[b], ACT.Sigmoid, stay[b])
         for b in range(BLOCKS):
-            product("cand%d" % b, 2 - 2 * b, cand[b], ACT.Tanh, neg_cand[b])
+            product("cand%d" % b, BLOCKS + b, cand[b], ACT.Tanh, neg_cand[b])
 
         kept = [sbuf([P, S], F32, "kept%d" % b) for b in range(BLOCKS)]
         fresh = [sbuf([P, S], F32, "fresh%d" % b) for b in range(BLOCKS)]
-        old1 = sbuf([P, S], F32, "old1")
+        old1 = sbuf([P, SCALAR_GATHERS], F32, "old1")
         new0 = [sbuf([P, HALF], F32, "new0_%d" % h) for h in range(2)]
+        halves = [slice(h * HALF, (h + 1) * HALF) for h in range(2)]
 
-        def gate_times_candidate(b):
+        def entries(cols):
+            return slot_sb[:, cols.start // LIST_ROWS : cols.stop // LIST_ROWS]
+
+        def gate_times_candidate(b, cols):
             nc.vector.scalar_tensor_tensor(
-                out=fresh[b][:], in0=stay[b][:], scalar=1.0, in1=neg_cand[b][:], op0=ALU.subtract, op1=ALU.mult
+                out=fresh[b][:, cols],
+                in0=stay[b][:, cols],
+                scalar=1.0,
+                in1=neg_cand[b][:, cols],
+                op0=ALU.subtract,
+                op1=ALU.mult,
             )
 
-        def scatter_half(h):
-            cols = slice(h * HALF, (h + 1) * HALF)
-            offsets = slot_sb[:, h * HALF // LIST_ROWS : (h + 1) * HALF // LIST_ROWS]
+        by_scalar, by_vector = slice(0, SCALAR_GATHERS), slice(SCALAR_GATHERS, S)
+        old0 = sbuf([P, HALF], F32, "old0")
+        nc.vector.tensor_copy(old0[:], window[0][:].indirect(entries(halves[0])))
+        nc.vector.tensor_tensor(
+            kept[0][:, halves[1]], window[0][:].indirect(entries(halves[1])), stay[0][:, halves[1]], ALU.mult
+        )
+        nc.vector.tensor_tensor(kept[0][:, halves[0]], old0[:], stay[0][:, halves[0]], ALU.mult)
+        nc.scalar.activation(out=old1[:], in_=window[1][:].indirect(entries(by_scalar)), func=ACT.Copy)
+        for cols in halves:
+            gate_times_candidate(0, cols)
+        for h, cols in enumerate(halves):
             nc.vector.tensor_tensor(new0[h][:], kept[0][:, cols], fresh[0][:, cols], ALU.add)
-            nc.scalar.activation(out=window[0][:].indirect(offsets), in_=new0[h][:], func=ACT.Copy)
-
-        nc.vector.tensor_tensor(kept[0][:], window[0][:].indirect(slot_sb[:]), stay[0][:], ALU.mult)
-        nc.scalar.activation(out=old1[:], in_=window[1][:].indirect(slot_sb[:]), func=ACT.Copy)
-        gate_times_candidate(0)
-        gate_times_candidate(1)
-        scatter_half(0)
-        nc.vector.tensor_tensor(kept[1][:], old1[:], stay[1][:], ALU.mult)
-        scatter_half(1)
+            nc.scalar.activation(out=window[0][:].indirect(entries(cols)), in_=new0[h][:], func=ACT.Copy)
         nc.sync.dma_start(out[rows_of(0), :], window[0][:])
+        nc.vector.tensor_tensor(
+            kept[1][:, by_vector], window[1][:].indirect(entries(by_vector)), stay[1][:, by_vector], ALU.mult
+        )
+        gate_times_candidate(1, slice(0, S))
+        nc.vector.tensor_tensor(kept[1][:, by_scalar], old1[:], stay[1][:, by_scalar], ALU.mult)
         nc.vector.tensor_tensor(window[1][:].indirect(slot_sb[:]), kept[1][:], fresh[1][:], ALU.add)
         nc.sync.dma_start(out[rows_of(1), :], window[1][:])

@@ -26,7 +26,7 @@ SCALE_ROWS = 4
 RUN = 4
 LIST_ROWS = 16
 HALF = S // 2
-SCALAR_GATHERS = 384
+SCALAR_GATHERS = 320
 ROW_BYTES = 4 * U
 
 
@@ -117,20 +117,23 @@ def tile_picked_gmem_tanh_p_kernel(
             interleave(nc.scalar.copy, grouped_first[b][:], raw[0][:, :, rows_of(b)])
         gate_first = [quantise("gate%d_pass0" % b, grouped_first[b])[0] for b in range(BLOCKS)]
         nc.vector.tensor_copy(x_plane[1][:], scale_table[:, T:].indirect(offs_sb[:]))
-        gate_second = quantise("gate_pass1", interleave_on_scalar(1))
-        grouped_cand = [
-            [sbuf([P, P * PACK], BF16, "grouped_cand0_pass0"), over(4, [P, P * PACK], BF16, "grouped_cand1_pass0", at=4 * S - P * PACK)],
-            [sbuf([P, P * PACK], BF16, "grouped_cand%d_pass1" % b) for b in range(BLOCKS)],
-        ]
-        cand_by_pass = []
-        for z, copies in enumerate(((nc.scalar.copy, nc.scalar.copy), (nc.vector.tensor_copy, nc.scalar.copy))):
-            for b in range(BLOCKS):
-                interleave(copies[b], grouped_cand[z][b][:], raw[2 + z][:, :, rows_of(b)])
-            cand_by_pass.append([quantise("cand%d_pass%d" % (b, z), grouped_cand[z][b])[0] for b in range(BLOCKS)])
+        grouped_second = [sbuf([P, P * PACK], BF16, "grouped_second%d" % b) for b in range(BLOCKS)]
+        for b in range(BLOCKS):
+            interleave(nc.scalar.copy, grouped_second[b][:], raw[1][:, :, rows_of(b)])
+        gate_second = [quantise("gate%d_pass1" % b, grouped_second[b])[0] for b in range(BLOCKS)]
+        grouped_cand0 = [sbuf([P, P * PACK], BF16, "grouped_cand0_pass%d" % z) for z in range(PASSES)]
+        grouped_cand1 = sbuf([P, PASSES * P * PACK], BF16, "grouped_cand1")
+        interleave(nc.scalar.copy, grouped_cand0[0][:], raw[2][:, :, rows_of(0)])
+        interleave(nc.scalar.copy, grouped_cand1[:, grouped_part(0)], raw[2][:, :, rows_of(1)])
+        cut = P // 2
+        interleave(nc.vector.tensor_copy, grouped_cand0[1][:, : cut * PACK], raw[3][:, :, :cut])
+        interleave(nc.scalar.copy, grouped_cand0[1][:, cut * PACK :], raw[3][:, :, cut:P])
+        interleave(nc.vector.tensor_copy, grouped_cand1[:, grouped_part(1)], raw[3][:, :, rows_of(1)])
         gate = [[gate_first[b], gate_second[b]] for b in range(BLOCKS)]
-        cand = [[cand_by_pass[z][b] for z in range(PASSES)] for b in range(BLOCKS)]
+        cand0 = [quantise("cand0_pass%d" % z, grouped_cand0[z])[0] for z in range(PASSES)]
+        cand = [cand0, quantise("cand1", grouped_cand1)]
 
-        def product(name, bank, operands, func, result):
+        def product(name, bank, operands, func, result, pieces):
             acc = psum.tile([P, S], F32, name="acc_" + name, tag="bank%d" % bank)
             for z, (codes, plane) in enumerate(operands):
                 nc.tensor.matmul_mx(
@@ -142,20 +145,22 @@ def tile_picked_gmem_tanh_p_kernel(
                     start=(z == 0),
                     stop=(z == PASSES - 1),
                 )
-            nc.scalar.activation(out=result[:], in_=acc[:], func=func, scale=-1.0)
+            for cols in pieces:
+                nc.scalar.activation(out=result[:, cols], in_=acc[:, cols], func=func, scale=-1.0)
 
-        stay = [over(4, [P, S], F32, "stay%d" % b, at=4 * S * b) for b in range(BLOCKS)]
+        halves = [slice(h * HALF, (h + 1) * HALF) for h in range(2)]
+        pieces = [halves, [slice(0, S)]]
+        stay = [over(2, [P, S], F32, "stay%d" % b, at=4 * S * b) for b in range(BLOCKS)]
         neg_cand = [sbuf([P, S], F32, "neg_cand%d" % b) for b in range(BLOCKS)]
         for b in range(BLOCKS):
-            product("gate%d" % b, b, gate[b], ACT.Sigmoid, stay[b])
+            product("gate%d" % b, b, gate[b], ACT.Sigmoid, stay[b], pieces[b])
         for b in range(BLOCKS):
-            product("cand%d" % b, BLOCKS + b, cand[b], ACT.Tanh, neg_cand[b])
+            product("cand%d" % b, BLOCKS + b, cand[b], ACT.Tanh, neg_cand[b], pieces[b])
 
         kept = [sbuf([P, S], F32, "kept%d" % b) for b in range(BLOCKS)]
         fresh = [sbuf([P, S], F32, "fresh%d" % b) for b in range(BLOCKS)]
         old1 = sbuf([P, SCALAR_GATHERS], F32, "old1")
         new0 = [sbuf([P, HALF], F32, "new0_%d" % h) for h in range(2)]
-        halves = [slice(h * HALF, (h + 1) * HALF) for h in range(2)]
 
         def entries(cols):
             return slot_sb[:, cols.start // LIST_ROWS : cols.stop // LIST_ROWS]
@@ -171,23 +176,24 @@ def tile_picked_gmem_tanh_p_kernel(
             )
 
         by_scalar, by_vector = slice(0, SCALAR_GATHERS), slice(SCALAR_GATHERS, S)
-        old0 = sbuf([P, HALF], F32, "old0")
-        nc.vector.tensor_copy(old0[:], window[0][:].indirect(entries(halves[0])))
-        nc.vector.tensor_tensor(
-            kept[0][:, halves[1]], window[0][:].indirect(entries(halves[1])), stay[0][:, halves[1]], ALU.mult
-        )
-        nc.vector.tensor_tensor(kept[0][:, halves[0]], old0[:], stay[0][:, halves[0]], ALU.mult)
+        for cols in halves:
+            nc.vector.tensor_tensor(kept[0][:, cols], window[0][:].indirect(entries(cols)), stay[0][:, cols], ALU.mult)
         nc.scalar.activation(out=old1[:], in_=window[1][:].indirect(entries(by_scalar)), func=ACT.Copy)
         for cols in halves:
             gate_times_candidate(0, cols)
-        for h, cols in enumerate(halves):
+
+        def add_and_scatter(h):
+            cols = halves[h]
             nc.vector.tensor_tensor(new0[h][:], kept[0][:, cols], fresh[0][:, cols], ALU.add)
             nc.scalar.activation(out=window[0][:].indirect(entries(cols)), in_=new0[h][:], func=ACT.Copy)
-        nc.sync.dma_start(out[rows_of(0), :], window[0][:])
+
+        add_and_scatter(0)
         nc.vector.tensor_tensor(
             kept[1][:, by_vector], window[1][:].indirect(entries(by_vector)), stay[1][:, by_vector], ALU.mult
         )
         gate_times_candidate(1, slice(0, S))
         nc.vector.tensor_tensor(kept[1][:, by_scalar], old1[:], stay[1][:, by_scalar], ALU.mult)
+        add_and_scatter(1)
+        nc.sync.dma_start(out[rows_of(0), :], window[0][:])
         nc.vector.tensor_tensor(window[1][:].indirect(slot_sb[:]), kept[1][:], fresh[1][:], ALU.add)
         nc.sync.dma_start(out[rows_of(1), :], window[1][:])

@@ -26,7 +26,7 @@ SCALE_ROWS = 4
 RUN = 4
 LIST_ROWS = 16
 HALF = S // 2
-SCALAR_GATHERS = 320
+SCALAR_GATHERS = 256
 ROW_BYTES = 4 * U
 
 
@@ -52,9 +52,9 @@ def tile_picked_gmem_tanh_p_kernel(
                 in_=raw.rearrange("p t (c i) -> p c t i", i=RUN),
             )
 
-        def quantise(name, grouped):
+        def quantise(name, grouped, codes=None):
             width = grouped.shape[1] // PACK
-            codes = sbuf([P, width], U32, "codes_" + name)
+            codes = codes if codes is not None else sbuf([P, width], U32, "codes_" + name)
             plane = sbuf([P, width], U8, "plane_" + name)
             nc.vector.quantize_mx(out=codes[:].bitcast(FP8X4), scales=plane[:], in_=grouped[:])
             return [(codes[:, lo : lo + P], plane[:, lo : lo + P]) for lo in range(0, width, P)]
@@ -108,54 +108,72 @@ def tile_picked_gmem_tanh_p_kernel(
             return grouped
 
         x_codes = [sbuf([P, S], U16, "x_codes%d" % z) for z in range(PASSES)]
-        x_plane = [sbuf([P, S], U8, "x_plane0"), over(0, [P, S], U8, "x_plane1")]
+        halves = [slice(h * HALF, (h + 1) * HALF) for h in range(2)]
+        plane_first = sbuf([P, S], U8, "x_plane0")
+        plane_second = [over(h, [P, HALF], U8, "x_plane1_half%d" % h) for h in range(2)]
+
+        def gather_second_plane(h):
+            offsets = offs_sb[:, h * HALF // LIST_ROWS : (h + 1) * HALF // LIST_ROWS]
+            nc.vector.tensor_copy(plane_second[h][:], scale_table[:, T:].indirect(offsets))
+
         for z in range(PASSES):
             nc.vector.tensor_copy(x_codes[z][:], word_table[z][:].indirect(offs_sb[:]))
-        nc.vector.tensor_copy(x_plane[0][:], scale_table[:, :T].indirect(offs_sb[:]))
+        nc.vector.tensor_copy(plane_first[:], scale_table[:, :T].indirect(offs_sb[:]))
         grouped_first = [sbuf([P, P * PACK], BF16, "grouped_first%d" % b) for b in range(BLOCKS)]
         for b in range(BLOCKS):
             interleave(nc.scalar.copy, grouped_first[b][:], raw[0][:, :, rows_of(b)])
         gate_first = [quantise("gate%d_pass0" % b, grouped_first[b])[0] for b in range(BLOCKS)]
-        nc.vector.tensor_copy(x_plane[1][:], scale_table[:, T:].indirect(offs_sb[:]))
+        gather_second_plane(0)
         grouped_second = [sbuf([P, P * PACK], BF16, "grouped_second%d" % b) for b in range(BLOCKS)]
         for b in range(BLOCKS):
             interleave(nc.scalar.copy, grouped_second[b][:], raw[1][:, :, rows_of(b)])
-        gate_second = [quantise("gate%d_pass1" % b, grouped_second[b])[0] for b in range(BLOCKS)]
-        grouped_cand0 = [sbuf([P, P * PACK], BF16, "grouped_cand0_pass%d" % z) for z in range(PASSES)]
-        grouped_cand1 = sbuf([P, PASSES * P * PACK], BF16, "grouped_cand1")
-        interleave(nc.scalar.copy, grouped_cand0[0][:], raw[2][:, :, rows_of(0)])
-        interleave(nc.scalar.copy, grouped_cand1[:, grouped_part(0)], raw[2][:, :, rows_of(1)])
-        cut = P // 2
-        interleave(nc.vector.tensor_copy, grouped_cand0[1][:, : cut * PACK], raw[3][:, :, :cut])
-        interleave(nc.scalar.copy, grouped_cand0[1][:, cut * PACK :], raw[3][:, :, cut:P])
-        interleave(nc.vector.tensor_copy, grouped_cand1[:, grouped_part(1)], raw[3][:, :, rows_of(1)])
+        gate_second = quantise("gate0_pass1", grouped_second[0])
+        gather_second_plane(1)
+        gate_second = gate_second + quantise("gate1_pass1", grouped_second[1])
+        grouped_cand = [[sbuf([P, P * PACK], BF16, "grouped_cand%d_pass%d" % (b, z)) for z in range(PASSES)] for b in range(BLOCKS)]
+        for b in range(BLOCKS):
+            interleave(nc.scalar.copy, grouped_cand[b][0][:], raw[2][:, :, rows_of(b)])
+        cand = [quantise("cand%d_pass0" % b, grouped_cand[b][0]) for b in range(BLOCKS)]
+        interleave(nc.scalar.copy, grouped_cand[0][1][:], raw[3][:, :, rows_of(0)])
+        interleave(nc.vector.tensor_copy, grouped_cand[1][1][:], raw[3][:, :, rows_of(1)])
+        cand[0] = cand[0] + quantise("cand0_pass1", grouped_cand[0][1])
+        cand[1] = cand[1] + quantise("cand1_pass1", grouped_cand[1][1], over(3, [P, P], U32, "codes_cand1_pass1"))
         gate = [[gate_first[b], gate_second[b]] for b in range(BLOCKS)]
-        cand0 = [quantise("cand0_pass%d" % z, grouped_cand0[z])[0] for z in range(PASSES)]
-        cand = [cand0, quantise("cand1", grouped_cand1)]
 
-        def product(name, bank, operands, func, result, pieces):
-            acc = psum.tile([P, S], F32, name="acc_" + name, tag="bank%d" % bank)
-            for z, (codes, plane) in enumerate(operands):
+        def product(name, operands, func, result, pieces):
+            (codes0, plane0), (codes1, plane1) = operands
+            accs = [psum.tile([P, c.stop - c.start], F32, name="acc_%s_%d" % (name, c.start)) for c in pieces]
+            for acc, cols in zip(accs, pieces):
                 nc.tensor.matmul_mx(
                     out=acc[:],
-                    lhsT=codes.bitcast(FP8X4),
-                    lhsT_scale=plane,
-                    rhs=x_codes[z][:].bitcast(FP4X4),
-                    rhs_scale=x_plane[z][:],
-                    start=(z == 0),
-                    stop=(z == PASSES - 1),
+                    lhsT=codes0.bitcast(FP8X4),
+                    lhsT_scale=plane0,
+                    rhs=x_codes[0][:, cols].bitcast(FP4X4),
+                    rhs_scale=plane_first[:, cols],
+                    start=True,
+                    stop=False,
                 )
-            for cols in pieces:
-                nc.scalar.activation(out=result[:, cols], in_=acc[:, cols], func=func, scale=-1.0)
+            for acc, cols in zip(accs, pieces):
+                inside = [h for h in range(2) if cols.start <= halves[h].start < cols.stop]
+                for h in inside:
+                    nc.tensor.matmul_mx(
+                        out=acc[:, halves[h].start - cols.start : halves[h].stop - cols.start],
+                        lhsT=codes1.bitcast(FP8X4),
+                        lhsT_scale=plane1,
+                        rhs=x_codes[1][:, halves[h]].bitcast(FP4X4),
+                        rhs_scale=plane_second[h][:],
+                        start=False,
+                        stop=(h == inside[-1]),
+                    )
+                nc.scalar.activation(out=result[:, cols], in_=acc[:], func=func, scale=-1.0)
 
-        halves = [slice(h * HALF, (h + 1) * HALF) for h in range(2)]
         pieces = [halves, [slice(0, S)]]
         stay = [over(2, [P, S], F32, "stay%d" % b, at=4 * S * b) for b in range(BLOCKS)]
         neg_cand = [sbuf([P, S], F32, "neg_cand%d" % b) for b in range(BLOCKS)]
         for b in range(BLOCKS):
-            product("gate%d" % b, b, gate[b], ACT.Sigmoid, stay[b], pieces[b])
+            product("gate%d" % b, gate[b], ACT.Sigmoid, stay[b], pieces[b])
         for b in range(BLOCKS):
-            product("cand%d" % b, BLOCKS + b, cand[b], ACT.Tanh, neg_cand[b], pieces[b])
+            product("cand%d" % b, cand[b], ACT.Tanh, neg_cand[b], pieces[b])
 
         kept = [sbuf([P, S], F32, "kept%d" % b) for b in range(BLOCKS)]
         fresh = [sbuf([P, S], F32, "fresh%d" % b) for b in range(BLOCKS)]

@@ -86,8 +86,8 @@ def tile_picked_gmem_tanh_p_kernel(
         def load_words(z):
             nc.sync.dma_start(word_table[z][:].bitcast(I32), x_words[z].bitcast(I32))
 
-        nc.sync.dma_start(offs_sb[:], offs)
         load_words(0)
+        nc.sync.dma_start(offs_sb[:], offs)
         load_words(1)
         for q in range(P // QUAD):
             nc.sync.dma_start(

@@ -23,7 +23,7 @@ PASSES = K // K_PASS
 BLOCKS = N // P
 QUAD = 32
 SCALE_ROWS = 4
-RUN = 4
+RUN = 2
 LIST_ROWS = 16
 HALF = S // 2
 SCALAR_GATHERS = 256

@@ -27,6 +27,7 @@ RUN = 2
 LIST_ROWS = 16
 HALF = S // 2
 SCALAR_GATHERS = 256
+ALIGN = 256
 ROW_BYTES = 4 * U
 
 
@@ -41,7 +42,7 @@ def tile_picked_gmem_tanh_p_kernel(
         psum = ctx.enter_context(tc.psum_pool(name="psum", bufs=1))
 
         def sbuf(shape, dtype, name, buffer_of=None):
-            return keep.tile(shape, dtype, name=name, tag=buffer_of or name, align_bytes=64)
+            return keep.tile(shape, dtype, name=name, tag=buffer_of or name, align_bytes=ALIGN)
 
         def load_weights(raw, w, z):
             nc.sync.dma_start(raw, w[z * K_PASS : (z + 1) * K_PASS, :].rearrange("(p t) m -> p t m", t=PACK))
@@ -66,7 +67,7 @@ def tile_picked_gmem_tanh_p_kernel(
             return slice(i * P * PACK, (i + 1) * P * PACK)
 
         def over(raw_index, shape, dtype, name, at=0):
-            return placed.tile(shape, dtype, name=name, offset=raw_index * ROW_BYTES + at, align_bytes=64)
+            return placed.tile(shape, dtype, name=name, offset=raw_index * ROW_BYTES + at, align_bytes=ALIGN)
 
         scale_table = sbuf([P, PASSES * T], U8, "scale_table")
         nc.vector.memset(scale_table[:].bitcast(I32), 0)

@@ -26,7 +26,7 @@ SCALE_ROWS = 4
 RUN = 2
 LIST_ROWS = 16
 HALF = S // 2
-SCALAR_GATHERS = 256
+SCALAR_GATHERS = 288
 ALIGN = 256
 ROW_BYTES = 4 * U
 
@@ -96,9 +96,9 @@ def tile_picked_gmem_tanh_p_kernel(
                 x_scales[:, SCALE_ROWS * q : SCALE_ROWS * (q + 1), :].bitcast(I32).rearrange("z r c -> r z c"),
             )
         load_weights(raw[0][:], *sources[0])
-        nc.sync.dma_start(slot_sb[:], slot)
         for i in range(1, len(sources)):
             load_weights(raw[i][:], *sources[i])
+        nc.sync.dma_start(slot_sb[:], slot)
         for b in range(BLOCKS):
             nc.sync.dma_start(window[b][:], mem[rows_of(b), :])
 

@@ -102,12 +102,6 @@ def tile_picked_gmem_tanh_p_kernel(
         for b in range(BLOCKS):
             nc.sync.dma_start(window[b][:], mem[rows_of(b), :])
 
-        def interleave_on_scalar(i):
-            grouped = sbuf([P, N * PACK], BF16, "grouped%d" % i)
-            for b in range(BLOCKS):
-                interleave(nc.scalar.copy, grouped[:, grouped_part(b)], raw[i][:, :, rows_of(b)])
-            return grouped
-
         x_codes = [sbuf([P, S], U16, "x_codes%d" % z) for z in range(PASSES)]
         halves = [slice(h * HALF, (h + 1) * HALF) for h in range(2)]
         plane_first = sbuf([P, S], U8, "x_plane0")
@@ -121,8 +115,15 @@ def tile_picked_gmem_tanh_p_kernel(
             nc.vector.tensor_copy(x_codes[z][:], word_table[z][:].indirect(offs_sb[:]))
         nc.vector.tensor_copy(plane_first[:], scale_table[:, :T].indirect(offs_sb[:]))
         grouped_first = [sbuf([P, P * PACK], BF16, "grouped_first%d" % b) for b in range(BLOCKS)]
-        for b in range(BLOCKS):
-            interleave(nc.scalar.copy, grouped_first[b][:], raw[0][:, :, rows_of(b)])
+        interleave(nc.scalar.copy, grouped_first[0][:], raw[0][:, :, rows_of(0)])
+        nc.gpsimd.tensor_scalar(
+            grouped_first[1][:].rearrange("p (m t) -> p m t", t=PACK),
+            raw[0][:, :, rows_of(1)].rearrange("p t m -> p m t"),
+            1.0,
+            0.0,
+            ALU.mult,
+            ALU.add,
+        )
         gate_first = [quantise("gate%d_pass0" % b, grouped_first[b])[0] for b in range(BLOCKS)]
         gather_second_plane(0)
         grouped_second = [sbuf([P, P * PACK], BF16, "grouped_second%d" % b) for b in range(BLOCKS)]

from contextlib import ExitStack

import concourse.mybir as mybir

K, T, S, N, U = 1024, 1024, 512, 256, 1024
FLOPS = 2 * 2 * K * N * S

F32 = mybir.dt.float32
BF16 = mybir.dt.bfloat16
I32 = mybir.dt.int32
U32 = mybir.dt.uint32
U16 = mybir.dt.uint16
U8 = mybir.dt.uint8
FP8X4 = mybir.dt.float8_e4m3fn_x4
FP4X4 = mybir.dt.float4_e2m1fn_x4
ACT = mybir.ActivationFunctionType
ALU = mybir.AluOpType

P = 128
PACK = 4
K_PASS = P * PACK
PASSES = K // K_PASS
BLOCKS = N // P
QUAD = 32
SCALE_ROWS = 4
RUN = 2
LIST_ROWS = 16
HALF = S // 2
SCALAR_GATHERS = 288
ALIGN = 256
ROW_BYTES = 4 * U


def tile_picked_gmem_tanh_p_kernel(
    tc, x_words, x_scales, mem, w1, w2, offs, slot, out
):
    nc = tc.nc
    with ExitStack() as ctx:
        lists = ctx.enter_context(tc.tile_pool(name="lists", bufs=1))
        keep = ctx.enter_context(tc.tile_pool(name="keep", bufs=1))
        placed = ctx.enter_context(tc.tile_pool(name="placed", bufs=1))
        psum = ctx.enter_context(tc.psum_pool(name="psum", bufs=1))

        def sbuf(shape, dtype, name, buffer_of=None):
            return keep.tile(shape, dtype, name=name, tag=buffer_of or name, align_bytes=ALIGN)

        def load_weights(raw, w, z):
            nc.sync.dma_start(raw, w[z * K_PASS : (z + 1) * K_PASS, :].rearrange("(p t) m -> p t m", t=PACK))

        def interleave(engine_copy, grouped, raw):
            engine_copy(
                out=grouped.rearrange("p (c i t) -> p c t i", i=RUN, t=PACK),
                in_=raw.rearrange("p t (c i) -> p c t i", i=RUN),
            )

        def quantise(name, grouped, codes=None):
            width = grouped.shape[1] // PACK
            codes = codes if codes is not None else sbuf([P, width], U32, "codes_" + name)
            plane = sbuf([P, width], U8, "plane_" + name)
            nc.vector.quantize_mx(out=codes[:].bitcast(FP8X4), scales=plane[:], in_=grouped[:])
            return [(codes[:, lo : lo + P], plane[:, lo : lo + P]) for lo in range(0, width, P)]

        def rows_of(b):
            return slice(b * P, (b + 1) * P)

        def grouped_part(i):
            return slice(i * P * PACK, (i + 1) * P * PACK)

        def over(raw_index, shape, dtype, name, at=0):
            return placed.tile(shape, dtype, name=name, offset=raw_index * ROW_BYTES + at, align_bytes=ALIGN)

        scale_table = sbuf([P, PASSES * T], U8, "scale_table")
        nc.vector.memset(scale_table[:].bitcast(I32), 0)

        warm_in = sbuf([P, 1], F32, "warm_in")
        warm_out = sbuf([P, 1], F32, "warm_out")
        nc.vector.memset(warm_in[:], 0.0)
        nc.scalar.activation(out=warm_out[:], in_=warm_in[:], func=ACT.Sigmoid)

        offs_sb = lists.tile([P, S // LIST_ROWS], U16, name="offs_sb")
        slot_sb = lists.tile([P, S // LIST_ROWS], U16, name="slot_sb")
        word_table = [sbuf([P, T], U16, "word_table%d" % z) for z in range(PASSES)]
        sources = [(w2, 0), (w2, 1), (w1, 0), (w1, 1)]
        raw = [over(i, [P, PACK, N], F32, "raw%d" % i) for i in range(len(sources))]
        window = [sbuf([P, U], F32, "window%d" % b) for b in range(BLOCKS)]

        def load_words(z):
            nc.sync.dma_start(word_table[z][:].bitcast(I32), x_words[z].bitcast(I32))

        load_words(0)
        nc.sync.dma_start(offs_sb[:], offs)
        load_words(1)
        for q in range(P // QUAD):
            nc.sync.dma_start(
                scale_table[QUAD * q : QUAD * q + SCALE_ROWS, :].bitcast(I32).rearrange("r (z c) -> r z c", z=PASSES),
                x_scales[:, SCALE_ROWS * q : SCALE_ROWS * (q + 1), :].bitcast(I32).rearrange("z r c -> r z c"),
            )
        load_weights(raw[0][:], *sources[0])
        for i in range(1, len(sources)):
            load_weights(raw[i][:], *sources[i])
        nc.sync.dma_start(slot_sb[:], slot)
        for b in range(BLOCKS):
            nc.sync.dma_start(window[b][:], mem[rows_of(b), :])

        x_codes = [sbuf([P, S], U16, "x_codes%d" % z) for z in range(PASSES)]
        halves = [slice(h * HALF, (h + 1) * HALF) for h in range(2)]
        plane_first = sbuf([P, S], U8, "x_plane0")
        plane_second = [over(h, [P, HALF], U8, "x_plane1_half%d" % h) for h in range(2)]

        def gather_second_plane(h):
            offsets = offs_sb[:, h * HALF // LIST_ROWS : (h + 1) * HALF // LIST_ROWS]
            nc.vector.tensor_copy(plane_second[h][:], scale_table[:, T:].indirect(offsets))

        for z in range(PASSES):
            nc.vector.tensor_copy(x_codes[z][:], word_table[z][:].indirect(offs_sb[:]))
        nc.vector.tensor_copy(plane_first[:], scale_table[:, :T].indirect(offs_sb[:]))
        grouped_first = [sbuf([P, P * PACK], BF16, "grouped_first%d" % b) for b in range(BLOCKS)]
        interleave(nc.scalar.copy, grouped_first[0][:], raw[0][:, :, rows_of(0)])
        nc.gpsimd.tensor_scalar(
            grouped_first[1][:].rearrange("p (m t) -> p m t", t=PACK),
            raw[0][:, :, rows_of(1)].rearrange("p t m -> p m t"),
            1.0,
            0.0,
            ALU.mult,
            ALU.add,
        )
        gate_first = [quantise("gate%d_pass0" % b, grouped_first[b])[0] for b in range(BLOCKS)]
        gather_second_plane(0)
        grouped_second = [sbuf([P, P * PACK], BF16, "grouped_second%d" % b) for b in range(BLOCKS)]
        for b in range(BLOCKS):
            interleave(nc.scalar.copy, grouped_second[b][:], raw[1][:, :, rows_of(b)])
        gate_second = quantise("gate0_pass1", grouped_second[0])
        gather_second_plane(1)
        gate_second = gate_second + quantise("gate1_pass1", grouped_second[1])
        grouped_cand = [[sbuf([P, P * PACK], BF16, "grouped_cand%d_pass%d" % (b, z)) for z in range(PASSES)] for b in range(BLOCKS)]
        for b in range(BLOCKS):
            interleave(nc.scalar.copy, grouped_cand[b][0][:], raw[2][:, :, rows_of(b)])
        cand = [quantise("cand%d_pass0" % b, grouped_cand[b][0]) for b in range(BLOCKS)]
        interleave(nc.scalar.copy, grouped_cand[0][1][:], raw[3][:, :, rows_of(0)])
        interleave(nc.vector.tensor_copy, grouped_cand[1][1][:], raw[3][:, :, rows_of(1)])
        cand[0] = cand[0] + quantise("cand0_pass1", grouped_cand[0][1])
        cand[1] = cand[1] + quantise("cand1_pass1", grouped_cand[1][1], over(3, [P, P], U32, "codes_cand1_pass1"))
        gate = [[gate_first[b], gate_second[b]] for b in range(BLOCKS)]

        def product(name, operands, func, result, pieces):
            (codes0, plane0), (codes1, plane1) = operands
            accs = [psum.tile([P, c.stop - c.start], F32, name="acc_%s_%d" % (name, c.start)) for c in pieces]
            for acc, cols in zip(accs, pieces):
                nc.tensor.matmul_mx(
                    out=acc[:],
                    lhsT=codes0.bitcast(FP8X4),
                    lhsT_scale=plane0,
                    rhs=x_codes[0][:, cols].bitcast(FP4X4),
                    rhs_scale=plane_first[:, cols],
                    start=True,
                    stop=False,
                )
            for acc, cols in zip(accs, pieces):
                inside = [h for h in range(2) if cols.start <= halves[h].start < cols.stop]
                for h in inside:
                    nc.tensor.matmul_mx(
                        out=acc[:, halves[h].start - cols.start : halves[h].stop - cols.start],
                        lhsT=codes1.bitcast(FP8X4),
                        lhsT_scale=plane1,
                        rhs=x_codes[1][:, halves[h]].bitcast(FP4X4),
                        rhs_scale=plane_second[h][:],
                        start=False,
                        stop=(h == inside[-1]),
                    )
                nc.scalar.activation(out=result[:, cols], in_=acc[:], func=func, scale=-1.0)

        pieces = [halves, [slice(0, S)]]
        stay = [over(2, [P, S], F32, "stay%d" % b, at=4 * S * b) for b in range(BLOCKS)]
        neg_cand = [sbuf([P, S], F32, "neg_cand%d" % b) for b in range(BLOCKS)]
        for b in range(BLOCKS):
            product("gate%d" % b, gate[b], ACT.Sigmoid, stay[b], pieces[b])
        for b in range(BLOCKS):
            product("cand%d" % b, cand[b], ACT.Tanh, neg_cand[b], pieces[b])

        kept = [sbuf([P, S], F32, "kept%d" % b) for b in range(BLOCKS)]
        fresh = [sbuf([P, S], F32, "fresh%d" % b) for b in range(BLOCKS)]
        old1 = sbuf([P, SCALAR_GATHERS], F32, "old1")
        new0 = [sbuf([P, HALF], F32, "new0_%d" % h) for h in range(2)]

        def entries(cols):
            return slot_sb[:, cols.start // LIST_ROWS : cols.stop // LIST_ROWS]

        def gate_times_candidate(b, cols):
            nc.vector.scalar_tensor_tensor(
                out=fresh[b][:, cols],
                in0=stay[b][:, cols],
                scalar=1.0,
                in1=neg_cand[b][:, cols],
                op0=ALU.subtract,
                op1=ALU.mult,
            )

        by_scalar, by_vector = slice(0, SCALAR_GATHERS), slice(SCALAR_GATHERS, S)
        for cols in halves:
            nc.vector.tensor_tensor(kept[0][:, cols], window[0][:].indirect(entries(cols)), stay[0][:, cols], ALU.mult)
        nc.scalar.activation(out=old1[:], in_=window[1][:].indirect(entries(by_scalar)), func=ACT.Copy)
        for cols in halves:
            gate_times_candidate(0, cols)

        def add_and_scatter(h):
            cols = halves[h]
            nc.vector.tensor_tensor(new0[h][:], kept[0][:, cols], fresh[0][:, cols], ALU.add)
            nc.scalar.activation(out=window[0][:].indirect(entries(cols)), in_=new0[h][:], func=ACT.Copy)

        add_and_scatter(0)
        nc.vector.tensor_tensor(
            kept[1][:, by_vector], window[1][:].indirect(entries(by_vector)), stay[1][:, by_vector], ALU.mult
        )
        gate_times_candidate(1, slice(0, S))
        nc.vector.tensor_tensor(kept[1][:, by_scalar], old1[:], stay[1][:, by_scalar], ALU.mult)
        add_and_scatter(1)
        nc.sync.dma_start(out[rows_of(0), :], window[0][:])
        nc.vector.tensor_tensor(window[1][:].indirect(slot_sb[:]), kept[1][:], fresh[1][:], ALU.add)
        nc.sync.dma_start(out[rows_of(1), :], window[1][:])
